import numpy as np
import ml_dtypes


def mxq(x, axis, fmt="e4m3"):
    dtype, down = {"e4m3": (ml_dtypes.float8_e4m3fn, 7), "e5m2": (ml_dtypes.float8_e5m2, 14)}[fmt]
    v = np.moveaxis(np.asarray(x, np.float32).astype(ml_dtypes.bfloat16).astype(np.float64), axis, -1)
    blocks = v.reshape(v.shape[:-1] + (-1, 32))
    amax = np.abs(blocks).max(-1, keepdims=True)
    byte = np.maximum(np.where(amax > 0, np.frexp(amax)[1] - 1 + 127, 0) - down, 1)
    scale = np.exp2(byte - 127.0)
    codes = (blocks / scale).astype(np.float32).astype(dtype).astype(np.float64)
    return np.moveaxis((codes * scale).reshape(v.shape), -1, axis)


WIDE = False


def mx_kscale(k):
    if not WIDE:
        return np.ones(k)
    levels = np.array([30, -30])
    if k % 512:
        return np.exp2(np.random.permutation(np.resize(levels, k // 32))).repeat(32)
    a = np.empty((k // 512, 16))
    for p in range(k // 512):
        a[p, :8] = np.random.permutation(np.resize(levels, 8))
        for g in range(8):
            far = levels[np.abs(levels - a[p, g]) >= 10]
            a[p, g + 8] = far[np.random.randint(len(far))]
    return np.exp2(a.ravel()).repeat(32)


def f64(x):
    return np.asarray(x).astype(np.float64)


def planes(y):
    n, m = y.shape
    v = y.astype(np.float32).astype(ml_dtypes.bfloat16).astype(np.float64).reshape(n // 32, 32, m)
    top = np.abs(v).max(1)
    byte = np.clip(np.where(top > 0, np.frexp(top)[1] - 1 + 127 - 7, 1), 1, 254)
    codes = (v * np.exp2(127.0 - byte)[:, None, :]).reshape(n, m).astype(np.float32).astype(ml_dtypes.float8_e4m3fn).view(np.uint8)
    words = codes.reshape(n // 512, 128, 4, m).transpose(0, 1, 3, 2)
    return np.ascontiguousarray(words), np.ascontiguousarray(byte.astype(np.uint8).reshape(n // 512, 16, m))


K, M, T = 1536, 1536, 512


def setup_inputs():
    n = np.random.standard_normal
    s1 = mx_kscale(K)[:, None]
    s2 = mx_kscale(K)[:, None]
    return {
        "w": (n((K, M)) / np.sqrt(K) * s1).astype(np.float32),
        "xd": (n((K, T)) / s1).astype(np.float32),
        "wd": (n((K, M)) / np.sqrt(K) * s2).astype(np.float32),
        "x": (n((K, T)) / s2).astype(np.float32),
        "g": (n((1536, 512))).astype(np.float32),
    }


def reference(w, xd, wd, x, g):
    w_ = mxq(f64(w), 0, "e4m3")
    xd_ = mxq(f64(xd), 0, "e5m2")
    wd_ = mxq(f64(wd), 0, "e5m2")
    x_ = mxq(f64(x), 0, "e4m3")
    y = w_.T @ xd_ + wd_.T @ x_
    out_0 = f64(g) * y
    return (out_0,) + planes(out_0)

@@ -1,0 +1,225 @@
+from contextlib import ExitStack
+
+import concourse.mybir as mybir
+
+K, M, T = 1536, 1536, 512
+FLOPS = 2 * 2 * K * M * T
+
+F32 = mybir.dt.float32
+BF16 = mybir.dt.bfloat16
+U32 = mybir.dt.uint32
+I32 = mybir.dt.int32
+U8 = mybir.dt.uint8
+E4M3 = mybir.dt.float8_e4m3fn_x4
+E5M2 = mybir.dt.float8_e5m2_x4
+
+P = 128
+PACK = 4
+SPAN = P * PACK
+GROUPS = M // SPAN
+STEPS = 2 * (K // SPAN)
+
+
+def tile_mix_jvp_fm_pl_mul_kernel(tc, w, xd, wd, x, g, out_0, out_1, out_2):
+    nc = tc.nc
+    on_vector = nc.vector.tensor_copy
+    on_scalar = nc.scalar.copy
+
+    weights = [w, wd]
+    moving = [xd, x]
+    weight_format = [E4M3, E5M2]
+    moving_format = [E5M2, E4M3]
+
+    with ExitStack() as ctx:
+        wide = ctx.enter_context(tc.tile_pool(name="wide", bufs=3))
+        narrow = ctx.enter_context(tc.tile_pool(name="narrow", bufs=3))
+        rounded = ctx.enter_context(tc.tile_pool(name="rounded", bufs=5))
+        keep = ctx.enter_context(tc.tile_pool(name="keep", bufs=1))
+        psum = ctx.enter_context(tc.psum_pool(name="psum", bufs=1))
+        ctx.enter_context(tc.manual_schedule())
+
+        raw = {}
+        bf = {}
+        codes = {}
+        scales = {}
+        acc = {}
+        res = {}
+
+        out_scales = keep.tile([P, GROUPS, T], U8, name="out_scales", align_bytes=64)
+
+        def rows(src, step):
+            c = step // 2
+            return src[c * SPAN : (c + 1) * SPAN, :].rearrange("(p j) n -> p j n", j=PACK)
+
+        def load_moving(step):
+            tile = narrow.tile([P, PACK, T], F32, name="x_raw_%d" % step, tag="narrow")
+            nc.sync.dma_start(out=tile[:], in_=rows(moving[step % 2], step))
+            raw["x", step] = tile[:]
+
+        def load_weights(step, first, count):
+            pool, tag = (narrow, "narrow") if count == 1 else (wide, "wide")
+            tile = pool.tile([P, PACK, count * SPAN], F32, name="w_raw_%d_%d" % (step, first), tag=tag)
+            cols = slice(first * SPAN, (first + count) * SPAN)
+            nc.sync.dma_start(out=tile[:], in_=rows(weights[step % 2], step)[:, :, cols])
+            for i in range(count):
+                raw["w", step, first + i] = tile[:, :, i * SPAN : (i + 1) * SPAN]
+
+        def load_g(a):
+            tile = keep.tile([P, PACK, T], F32, name="res_%d" % a)
+            nc.sync.dma_start(out=tile[:], in_=g[a * SPAN : (a + 1) * SPAN, :].rearrange("(p r) t -> p r t", r=PACK))
+            res[a] = tile
+
+        def round_plain(key, src, copy):
+            tile = rounded.tile([P, T * PACK], BF16, name="bf_" + "_".join(map(str, key)), tag="bf", align_bytes=64)
+            copy(
+                out=tile[:].rearrange("p (c i j) -> p c j i", i=4, j=PACK),
+                in_=src.rearrange("p j (c i) -> p c j i", i=4),
+            )
+            bf[key] = tile
+
+        def round_moving(step, copy):
+            round_plain(("x", step), raw["x", step], copy)
+
+        def round_result(a, copy):
+            round_plain(("o", a), res[a][:], copy)
+
+        def round_weights(step, a, copy):
+            key = ("w", step, a)
+            tile = rounded.tile([P, SPAN * PACK], BF16, name="bf_w_%d_%d" % (step, a), tag="bf", align_bytes=64)
+            copy(
+                out=tile[:].rearrange("p (r m j) -> p m j r", r=PACK, j=PACK),
+                in_=raw[key].rearrange("p j (m r) -> p m j r", r=PACK),
+            )
+            bf[key] = tile
+
+        def quantize(key, fmt, plane=None):
+            label = "_".join(map(str, key))
+            words = keep.tile([P, SPAN], U32, name="codes_" + label, align_bytes=64)
+            if plane is None:
+                own = keep.tile([P, SPAN], U8, name="scales_" + label, align_bytes=64)
+                plane = own[:]
+            nc.vector.quantize_mx(out=words[:].bitcast(fmt), scales=plane, in_=bf[key][:])
+            codes[key] = words
+            scales[key] = plane
+
+        def quantize_moving(step):
+            quantize(("x", step), moving_format[step % 2])
+
+        def quantize_weights(step, a):
+            quantize(("w", step, a), weight_format[step % 2])
+
+        def quantize_result(a):
+            quantize(("o", a), E4M3, out_scales[:, a, :])
+
+        def multiply(a, r, step, last):
+            first = (a, r) not in acc
+            if first:
+                bank = (a % 2) * PACK + r
+                acc[a, r] = psum.tile([P, T], F32, name="acc_%d_%d" % (a, r), tag="bank_%d" % bank)
+            cols = slice(r * P, (r + 1) * P)
+            nc.tensor.matmul_mx(
+                out=acc[a, r][:],
+                lhsT=codes["w", step, a][:, cols].bitcast(weight_format[step % 2]),
+                lhsT_scale=scales["w", step, a][:, cols],
+                rhs=codes["x", step][:].bitcast(moving_format[step % 2]),
+                rhs_scale=scales["x", step],
+                start=first,
+                stop=last,
+            )
+
+        def multiply_group(a, step, last=False):
+            for r in range(PACK):
+                multiply(a, r, step, last)
+
+        def gate(a, r):
+            nc.vector.tensor_tensor(
+                out=res[a][:, r, :], in0=acc[a, r][:], in1=res[a][:, r, :], op=mybir.AluOpType.mult
+            )
+
+        def store_result(a):
+            rows_out = out_0[a * SPAN : (a + 1) * SPAN, :].rearrange("(p r) t -> p r t", r=PACK)
+            nc.sync.dma_start(out=rows_out, in_=res[a][:])
+
+        def store_words(a):
+            dst = out_1[a].rearrange("p t i -> p (t i)").bitcast(I32)
+            nc.sync.dma_start(out=dst, in_=codes["o", a][:].bitcast(I32))
+
+        def store_scales():
+            for q in range(4):
+                dst = out_2[:, 4 * q : 4 * q + 4, :].rearrange("a r t -> r a t").bitcast(I32)
+                nc.scalar.dma_start(out=dst, in_=out_scales[32 * q : 32 * q + 4, :, :].bitcast(I32))
+
+        for step in range(3):
+            load_moving(step)
+            load_weights(step, 0, GROUPS)
+
+        round_moving(0, on_scalar)
+        quantize_moving(0)
+        for step in range(4):
+            round_weights(step, 0, on_vector)
+            round_weights(step, 1, on_scalar)
+            round_weights(step, 2, on_vector)
+            quantize_weights(step, 0)
+            multiply_group(0, step)
+            quantize_weights(step, 1)
+            multiply_group(1, step)
+            round_moving(step + 1, on_scalar)
+            quantize_weights(step, 2)
+            quantize_moving(step + 1)
+            if step == 0:
+                load_moving(3)
+                load_weights(3, 0, GROUPS)
+            if step == 1:
+                load_moving(4)
+                load_moving(5)
+            if step == 2:
+                load_weights(5, 0, 1)
+                load_weights(4, 0, GROUPS)
+                load_g(0)
+                load_weights(5, 1, 2)
+                load_g(1)
+                load_g(2)
+
+        round_moving(5, on_scalar)
+        quantize_moving(5)
+        round_weights(5, 0, on_scalar)
+        quantize_weights(5, 0)
+        multiply_group(0, 5)
+
+        round_weights(4, 0, on_vector)
+        round_weights(4, 1, on_scalar)
+        quantize_weights(4, 0)
+        multiply_group(0, 4, last=True)
+        round_weights(4, 2, on_scalar)
+        quantize_weights(4, 1)
+        multiply_group(1, 4)
+        for r in range(PACK):
+            gate(0, r)
+            for step in range(4):
+                multiply(2, r, step, False)
+        store_result(0)
+        quantize_weights(4, 2)
+        round_result(0, on_vector)
+        round_weights(5, 2, on_scalar)
+        round_weights(5, 1, on_vector)
+        quantize_result(0)
+        store_words(0)
+        quantize_weights(5, 1)
+        multiply_group(1, 5, last=True)
+        quantize_weights(5, 2)
+        for r in range(PACK):
+            multiply(2, r, 4, False)
+            multiply(2, r, 5, True)
+        for r in range(PACK):
+            gate(1, r)
+        store_result(1)
+        round_result(1, on_scalar)
+        for r in range(PACK):
+            gate(2, r)
+        store_result(2)
+        round_result(2, on_vector)
+        quantize_result(1)
+        store_words(1)
+        quantize_result(2)
+        store_words(2)
+        store_scales()

@@ -18,12 +18,17 @@ PACK = 4
 SPAN = P * PACK
 GROUPS = M // SPAN
 STEPS = 2 * (K // SPAN)
+SPLIT = 352
 
 
 def tile_mix_jvp_fm_pl_mul_kernel(tc, w, xd, wd, x, g, out_0, out_1, out_2):
     nc = tc.nc
     on_vector = nc.vector.tensor_copy
     on_scalar = nc.scalar.copy
+
+    all_vector = [(on_vector, 0, T)]
+    all_scalar = [(on_scalar, 0, T)]
+    both = [(on_scalar, SPLIT, T), (on_vector, 0, SPLIT)]
 
     weights = [w, wd]
     moving = [xd, x]
@@ -69,27 +74,29 @@ def tile_mix_jvp_fm_pl_mul_kernel(tc, w, xd, wd, x, g, out_0, out_1, out_2):
             nc.sync.dma_start(out=tile[:], in_=g[a * SPAN : (a + 1) * SPAN, :].rearrange("(p r) t -> p r t", r=PACK))
             res[a] = tile
 
-        def round_plain(key, src, copy):
+        def round_plain(key, src, shares):
             tile = rounded.tile([P, T * PACK], BF16, name="bf_" + "_".join(map(str, key)), tag="bf", align_bytes=64)
-            copy(
-                out=tile[:].rearrange("p (c i j) -> p c j i", i=4, j=PACK),
-                in_=src.rearrange("p j (c i) -> p c j i", i=4),
-            )
+            for copy, lo, hi in shares:
+                copy(
+                    out=tile[:, lo * PACK : hi * PACK].rearrange("p (c i j) -> p c j i", i=4, j=PACK),
+                    in_=src[:, :, lo:hi].rearrange("p j (c i) -> p c j i", i=4),
+                )
             bf[key] = tile
 
-        def round_moving(step, copy):
-            round_plain(("x", step), raw["x", step], copy)
+        def round_moving(step, shares):
+            round_plain(("x", step), raw["x", step], shares)
 
-        def round_result(a, copy):
-            round_plain(("o", a), res[a][:], copy)
+        def round_result(a, shares):
+            round_plain(("o", a), res[a][:], shares)
 
-        def round_weights(step, a, copy):
+        def round_weights(step, a, shares):
             key = ("w", step, a)
             tile = rounded.tile([P, SPAN * PACK], BF16, name="bf_w_%d_%d" % (step, a), tag="bf", align_bytes=64)
-            copy(
-                out=tile[:].rearrange("p (r m j) -> p m j r", r=PACK, j=PACK),
-                in_=raw[key].rearrange("p j (m r) -> p m j r", r=PACK),
-            )
+            dealt = tile[:].rearrange("p (r m j) -> p m j r", r=PACK, j=PACK)
+            source = raw[key].rearrange("p j (m r) -> p m j r", r=PACK)
+            for copy, lo, hi in shares:
+                part = slice(lo // PACK, hi // PACK)
+                copy(out=dealt[:, part], in_=source[:, part])
             bf[key] = tile
 
         def quantize(key, fmt, plane=None):
@@ -147,77 +154,72 @@ def tile_mix_jvp_fm_pl_mul_kernel(tc, w, xd, wd, x, g, out_0, out_1, out_2):
         def store_scales():
             for q in range(4):
                 dst = out_2[:, 4 * q : 4 * q + 4, :].rearrange("a r t -> r a t").bitcast(I32)
-                nc.scalar.dma_start(out=dst, in_=out_scales[32 * q : 32 * q + 4, :, :].bitcast(I32))
+                nc.sync.dma_start(out=dst, in_=out_scales[32 * q : 32 * q + 4, :, :].bitcast(I32))
 
         for step in range(3):
             load_moving(step)
             load_weights(step, 0, GROUPS)
 
-        round_moving(0, on_scalar)
+        round_moving(0, all_scalar)
         quantize_moving(0)
-        for step in range(4):
-            round_weights(step, 0, on_vector)
-            round_weights(step, 1, on_scalar)
-            round_weights(step, 2, on_vector)
+        for step in range(5):
+            round_weights(step, 0, all_vector)
+            round_weights(step, 1, all_scalar)
+            round_weights(step, 2, all_vector)
             quantize_weights(step, 0)
             multiply_group(0, step)
-            quantize_weights(step, 1)
-            multiply_group(1, step)
-            round_moving(step + 1, on_scalar)
+            if step < 4:
+                quantize_weights(step, 1)
+                multiply_group(1, step)
+                round_moving(step + 1, all_scalar)
             quantize_weights(step, 2)
-            quantize_moving(step + 1)
-            if step == 0:
-                load_moving(3)
-                load_weights(3, 0, GROUPS)
-            if step == 1:
-                load_moving(4)
-                load_moving(5)
+            if step < 4:
+                quantize_moving(step + 1)
+            if step < 2:
+                load_moving(step + 3)
+                load_weights(step + 3, 0, GROUPS)
             if step == 2:
-                load_weights(5, 0, 1)
-                load_weights(4, 0, GROUPS)
+                load_weights(5, 0, 2)
+                load_moving(5)
                 load_g(0)
-                load_weights(5, 1, 2)
+                load_weights(5, 2, 1)
                 load_g(1)
                 load_g(2)
 
-        round_moving(5, on_scalar)
-        quantize_moving(5)
-        round_weights(5, 0, on_scalar)
-        quantize_weights(5, 0)
-        multiply_group(0, 5)
-
-        round_weights(4, 0, on_vector)
-        round_weights(4, 1, on_scalar)
-        quantize_weights(4, 0)
-        multiply_group(0, 4, last=True)
-        round_weights(4, 2, on_scalar)
+        round_weights(5, 0, all_vector)
+        round_weights(5, 1, all_scalar)
         quantize_weights(4, 1)
         multiply_group(1, 4)
-        for r in range(PACK):
-            gate(0, r)
-            for step in range(4):
-                multiply(2, r, step, False)
-        store_result(0)
-        quantize_weights(4, 2)
-        round_result(0, on_vector)
-        round_weights(5, 2, on_scalar)
-        round_weights(5, 1, on_vector)
-        quantize_result(0)
-        store_words(0)
+        quantize_weights(5, 0)
+        round_moving(5, both)
+        quantize_moving(5)
+        multiply_group(0, 5, last=True)
         quantize_weights(5, 1)
         multiply_group(1, 5, last=True)
-        quantize_weights(5, 2)
         for r in range(PACK):
-            multiply(2, r, 4, False)
-            multiply(2, r, 5, True)
+            gate(0, r)
+        store_result(0)
+        round_result(0, all_scalar)
+        round_weights(5, 2, all_vector)
+        quantize_weights(5, 2)
+        for r in range(2):
+            for step in range(STEPS - 1):
+                multiply(2, r, step, False)
+        for r in range(2):
+            multiply(2, r, STEPS - 1, True)
+        for r in range(2, PACK):
+            for step in range(STEPS):
+                multiply(2, r, step, step == STEPS - 1)
         for r in range(PACK):
             gate(1, r)
         store_result(1)
-        round_result(1, on_scalar)
+        round_result(1, all_scalar)
+        quantize_result(0)
+        store_words(0)
         for r in range(PACK):
             gate(2, r)
         store_result(2)
-        round_result(2, on_vector)
+        round_result(2, both)
         quantize_result(1)
         store_words(1)
         quantize_result(2)

@@ -30,6 +30,8 @@ def tile_mix_jvp_fm_pl_mul_kernel(tc, w, xd, wd, x, g, out_0, out_1, out_2):
     all_scalar = [(on_scalar, 0, T)]
     both = [(on_scalar, SPLIT, T), (on_vector, 0, SPLIT)]
 
+    halves = [(on_scalar, T // 2, T), (on_vector, 0, T // 2)]
+
     weights = [w, wd]
     moving = [xd, x]
     weight_format = [E4M3, E5M2]
@@ -95,8 +97,8 @@ def tile_mix_jvp_fm_pl_mul_kernel(tc, w, xd, wd, x, g, out_0, out_1, out_2):
             dealt = tile[:].rearrange("p (r m j) -> p m j r", r=PACK, j=PACK)
             source = raw[key].rearrange("p j (m r) -> p m j r", r=PACK)
             for copy, lo, hi in shares:
-                part = slice(lo // PACK, hi // PACK)
-                copy(out=dealt[:, part], in_=source[:, part])
+                part = slice(lo // P, hi // P)
+                copy(out=dealt[:, :, :, part], in_=source[:, :, :, part])
             bf[key] = tile
 
         def quantize(key, fmt, plane=None):
@@ -152,9 +154,9 @@ def tile_mix_jvp_fm_pl_mul_kernel(tc, w, xd, wd, x, g, out_0, out_1, out_2):
             nc.sync.dma_start(out=dst, in_=codes["o", a][:].bitcast(I32))
 
         def store_scales():
-            for q in range(4):
-                dst = out_2[:, 4 * q : 4 * q + 4, :].rearrange("a r t -> r a t").bitcast(I32)
-                nc.sync.dma_start(out=dst, in_=out_scales[32 * q : 32 * q + 4, :, :].bitcast(I32))
+            for r in range(4):
+                dst = out_2.rearrange("a (q r) t -> r q a t", r=4)[r].bitcast(I32)
+                nc.sync.dma_start(out=dst, in_=out_scales[r:P:32, :, :].bitcast(I32))
 
         for step in range(3):
             load_moving(step)
@@ -199,8 +201,8 @@ def tile_mix_jvp_fm_pl_mul_kernel(tc, w, xd, wd, x, g, out_0, out_1, out_2):
         for r in range(PACK):
             gate(0, r)
         store_result(0)
+        round_weights(5, 2, halves)
         round_result(0, all_scalar)
-        round_weights(5, 2, all_vector)
         quantize_weights(5, 2)
         for r in range(2):
             for step in range(STEPS - 1):

@@ -19,6 +19,8 @@ SPAN = P * PACK
 GROUPS = M // SPAN
 STEPS = 2 * (K // SPAN)
 SPLIT = 352
+HELD = 256
+LATE_ROWS = 2
 
 
 def tile_mix_jvp_fm_pl_mul_kernel(tc, w, xd, wd, x, g, out_0, out_1, out_2):
@@ -30,6 +32,10 @@ def tile_mix_jvp_fm_pl_mul_kernel(tc, w, xd, wd, x, g, out_0, out_1, out_2):
     all_scalar = [(on_scalar, 0, T)]
     both = [(on_scalar, SPLIT, T), (on_vector, 0, SPLIT)]
 
+
+    def split_at(column):
+        return [(on_scalar, column, T), (on_vector, 0, column)]
+
     halves = [(on_scalar, T // 2, T), (on_vector, 0, T // 2)]
 
     weights = [w, wd]
@@ -40,7 +46,8 @@ def tile_mix_jvp_fm_pl_mul_kernel(tc, w, xd, wd, x, g, out_0, out_1, out_2):
     with ExitStack() as ctx:
         wide = ctx.enter_context(tc.tile_pool(name="wide", bufs=3))
         narrow = ctx.enter_context(tc.tile_pool(name="narrow", bufs=3))
-        rounded = ctx.enter_context(tc.tile_pool(name="rounded", bufs=5))
+        passing = ctx.enter_context(tc.tile_pool(name="passing", bufs=4))
+        rounded = ctx.enter_context(tc.tile_pool(name="rounded", bufs=6))
         keep = ctx.enter_context(tc.tile_pool(name="keep", bufs=1))
         psum = ctx.enter_context(tc.psum_pool(name="psum", bufs=1))
         ctx.enter_context(tc.manual_schedule())
@@ -71,19 +78,47 @@ def tile_mix_jvp_fm_pl_mul_kernel(tc, w, xd, wd, x, g, out_0, out_1, out_2):
             for i in range(count):
                 raw["w", step, first + i] = tile[:, :, i * SPAN : (i + 1) * SPAN]
 
+        def load_last_early():
+            tile = wide.tile([P, 6 * M], F32, name="w_raw_last", tag="wide")
+            flat = weights[1][(K - SPAN) :, :].rearrange("(p j) n -> p (j n)", j=PACK)
+            run = 2 * M + 2 * SPAN
+            nc.sync.dma_start(out=tile[:, :run], in_=flat[:, :run])
+            nc.sync.dma_start(out=tile[:, 3 * M : 3 * M + 2 * SPAN], in_=flat[:, 3 * M : 3 * M + 2 * SPAN])
+            view = tile[:].rearrange("p (j n) -> p j n", n=M)
+            for a in range(2):
+                raw["w", STEPS - 1, a] = view[:, :PACK, a * SPAN : (a + 1) * SPAN]
+            raw["last"] = view
+            raw["pairs"] = tile[:].rearrange("p (u v n) -> p u v n", u=2, v=3)
+
+        def load_last_late():
+            nc.sync.dma_start(out=raw["last"][:, 3:5, 2 * SPAN :], in_=rows(weights[1], STEPS - 1)[:, 2:, 2 * SPAN :])
+
+        def round_last():
+            key = ("w", STEPS - 1, 2)
+            tile = rounded.tile([P, SPAN * PACK], BF16, name="bf_w_last", tag="bf", align_bytes=64)
+            dealt = tile[:].rearrange("p (r m u v) -> p m u v r", r=PACK, u=2, v=2)
+            for copy, lo, hi in halves:
+                part = slice(lo // P, hi // P)
+                pairs = raw["pairs"][:, :, :2, 2 * SPAN :].rearrange("p u v (m r) -> p m u v r", r=PACK)
+                copy(out=dealt[:, :, :, :, part], in_=pairs[:, :, :, :, part])
+            bf[key] = tile
+
         def load_g(a):
             tile = keep.tile([P, PACK, T], F32, name="res_%d" % a)
             nc.sync.dma_start(out=tile[:], in_=g[a * SPAN : (a + 1) * SPAN, :].rearrange("(p r) t -> p r t", r=PACK))
             res[a] = tile
 
         def round_plain(key, src, shares):
-            tile = rounded.tile([P, T * PACK], BF16, name="bf_" + "_".join(map(str, key)), tag="bf", align_bytes=64)
+            if key not in bf:
+                bf[key] = rounded.tile(
+                    [P, T * PACK], BF16, name="bf_" + "_".join(map(str, key)), tag="bf", align_bytes=64
+                )
+            tile = bf[key]
             for copy, lo, hi in shares:
                 copy(
                     out=tile[:, lo * PACK : hi * PACK].rearrange("p (c i j) -> p c j i", i=4, j=PACK),
                     in_=src[:, :, lo:hi].rearrange("p j (c i) -> p c j i", i=4),
                 )
-            bf[key] = tile
 
         def round_moving(step, shares):
             round_plain(("x", step), raw["x", step], shares)
@@ -91,21 +126,25 @@ def tile_mix_jvp_fm_pl_mul_kernel(tc, w, xd, wd, x, g, out_0, out_1, out_2):
         def round_result(a, shares):
             round_plain(("o", a), res[a][:], shares)
 
-        def round_weights(step, a, shares):
+        def round_weights(step, a, shares, quads=slice(0, P)):
             key = ("w", step, a)
-            tile = rounded.tile([P, SPAN * PACK], BF16, name="bf_w_%d_%d" % (step, a), tag="bf", align_bytes=64)
+            if key not in bf:
+                bf[key] = rounded.tile(
+                    [P, SPAN * PACK], BF16, name="bf_w_%d_%d" % (step, a), tag="bf", align_bytes=64
+                )
+            tile = bf[key]
             dealt = tile[:].rearrange("p (r m j) -> p m j r", r=PACK, j=PACK)
             source = raw[key].rearrange("p j (m r) -> p m j r", r=PACK)
             for copy, lo, hi in shares:
                 part = slice(lo // P, hi // P)
-                copy(out=dealt[:, :, :, part], in_=source[:, :, :, part])
-            bf[key] = tile
+                copy(out=dealt[:, quads, :, part], in_=source[:, quads, :, part])
 
         def quantize(key, fmt, plane=None):
             label = "_".join(map(str, key))
-            words = keep.tile([P, SPAN], U32, name="codes_" + label, align_bytes=64)
+            home, tags = (passing, ("codes", "scales")) if key[0] == "w" and key[2] < 2 else (keep, (None, None))
+            words = home.tile([P, SPAN], U32, name="codes_" + label, tag=tags[0] or "codes_" + label, align_bytes=64)
             if plane is None:
-                own = keep.tile([P, SPAN], U8, name="scales_" + label, align_bytes=64)
+                own = home.tile([P, SPAN], U8, name="scales_" + label, tag=tags[1] or "scales_" + label, align_bytes=64)
                 plane = own[:]
             nc.vector.quantize_mx(out=words[:].bitcast(fmt), scales=plane, in_=bf[key][:])
             codes[key] = words
@@ -145,9 +184,9 @@ def tile_mix_jvp_fm_pl_mul_kernel(tc, w, xd, wd, x, g, out_0, out_1, out_2):
                 out=res[a][:, r, :], in0=acc[a, r][:], in1=res[a][:, r, :], op=mybir.AluOpType.mult
             )
 
-        def store_result(a):
+        def store_result(a, lo=0, hi=PACK):
             rows_out = out_0[a * SPAN : (a + 1) * SPAN, :].rearrange("(p r) t -> p r t", r=PACK)
-            nc.sync.dma_start(out=rows_out, in_=res[a][:])
+            nc.sync.dma_start(out=rows_out[:, lo:hi, :], in_=res[a][:, lo:hi, :])
 
         def store_words(a):
             dst = out_1[a].rearrange("p t i -> p (t i)").bitcast(I32)
@@ -164,36 +203,43 @@ def tile_mix_jvp_fm_pl_mul_kernel(tc, w, xd, wd, x, g, out_0, out_1, out_2):
 
         round_moving(0, all_scalar)
         quantize_moving(0)
-        for step in range(5):
+        for step in range(4):
             round_weights(step, 0, all_vector)
             round_weights(step, 1, all_scalar)
             round_weights(step, 2, all_vector)
             quantize_weights(step, 0)
             multiply_group(0, step)
-            if step < 4:
-                quantize_weights(step, 1)
-                multiply_group(1, step)
-                round_moving(step + 1, all_scalar)
+            quantize_weights(step, 1)
+            multiply_group(1, step)
+            round_moving(step + 1, all_scalar if step < 3 else [(on_scalar, 0, HELD)])
             quantize_weights(step, 2)
-            if step < 4:
+            if step < 3:
                 quantize_moving(step + 1)
             if step < 2:
                 load_moving(step + 3)
                 load_weights(step + 3, 0, GROUPS)
             if step == 2:
-                load_weights(5, 0, 2)
+                load_last_early()
                 load_moving(5)
                 load_g(0)
-                load_weights(5, 2, 1)
+                load_last_late()
                 load_g(1)
                 load_g(2)
 
-        round_weights(5, 0, all_vector)
-        round_weights(5, 1, all_scalar)
-        quantize_weights(4, 1)
+        round_weights(4, 0, all_vector)
+        round_weights(4, 1, all_scalar)
+        round_moving(4, [(on_scalar, HELD, T)])
+        round_weights(4, 2, all_vector)
+        for a in (0, 2, 1):
+            quantize_weights(4, a)
+        quantize_moving(4)
+        multiply_group(0, 4)
         multiply_group(1, 4)
+        round_weights(5, 0, all_vector)
+        round_weights(5, 1, all_scalar, slice(0, 96))
         quantize_weights(5, 0)
-        round_moving(5, both)
+        round_moving(5, split_at(352))
+        round_weights(5, 1, all_scalar, slice(96, P))
         quantize_moving(5)
         multiply_group(0, 5, last=True)
         quantize_weights(5, 1)
@@ -201,7 +247,7 @@ def tile_mix_jvp_fm_pl_mul_kernel(tc, w, xd, wd, x, g, out_0, out_1, out_2):
         for r in range(PACK):
             gate(0, r)
         store_result(0)
-        round_weights(5, 2, halves)
+        round_last()
         round_result(0, all_scalar)
         quantize_weights(5, 2)
         for r in range(2):
@@ -215,15 +261,18 @@ def tile_mix_jvp_fm_pl_mul_kernel(tc, w, xd, wd, x, g, out_0, out_1, out_2):
         for r in range(PACK):
             gate(1, r)
         store_result(1)
-        round_result(1, all_scalar)
+        round_result(1, split_at(128))
         quantize_result(0)
         store_words(0)
-        for r in range(PACK):
+        for r in range(PACK - 1):
             gate(2, r)
-        store_result(2)
-        round_result(2, both)
+            if r == 1:
+                store_result(2, 0, 2)
         quantize_result(1)
         store_words(1)
+        gate(2, PACK - 1)
+        store_result(2, 2, 4)
+        round_result(2, both)
         quantize_result(2)
         store_words(2)
         store_scales()

@@ -18,9 +18,14 @@ PACK = 4
 SPAN = P * PACK
 GROUPS = M // SPAN
 STEPS = 2 * (K // SPAN)
-SPLIT = 352
-HELD = 256
-LATE_ROWS = 2
+LAST = STEPS - 1
+LOADS_AHEAD = 3
+QUADRANT = 32
+HALF = T // 2
+
+EVEN_SHARE = 352
+HELP_SHARE = 128
+EARLY_QUADS = 96
 
 
 def tile_mix_jvp_fm_pl_mul_kernel(tc, w, xd, wd, x, g, out_0, out_1, out_2):
@@ -28,15 +33,10 @@ def tile_mix_jvp_fm_pl_mul_kernel(tc, w, xd, wd, x, g, out_0, out_1, out_2):
     on_vector = nc.vector.tensor_copy
     on_scalar = nc.scalar.copy
 
-    all_vector = [(on_vector, 0, T)]
     all_scalar = [(on_scalar, 0, T)]
-    both = [(on_scalar, SPLIT, T), (on_vector, 0, SPLIT)]
-
 
     def split_at(column):
         return [(on_scalar, column, T), (on_vector, 0, column)]
-
-    halves = [(on_scalar, T // 2, T), (on_vector, 0, T // 2)]
 
     weights = [w, wd]
     moving = [xd, x]
@@ -44,9 +44,8 @@ def tile_mix_jvp_fm_pl_mul_kernel(tc, w, xd, wd, x, g, out_0, out_1, out_2):
     moving_format = [E5M2, E4M3]
 
     with ExitStack() as ctx:
-        wide = ctx.enter_context(tc.tile_pool(name="wide", bufs=3))
-        narrow = ctx.enter_context(tc.tile_pool(name="narrow", bufs=3))
-        passing = ctx.enter_context(tc.tile_pool(name="passing", bufs=4))
+        wide = ctx.enter_context(tc.tile_pool(name="wide", bufs=LOADS_AHEAD))
+        narrow = ctx.enter_context(tc.tile_pool(name="narrow", bufs=LOADS_AHEAD))
         rounded = ctx.enter_context(tc.tile_pool(name="rounded", bufs=6))
         keep = ctx.enter_context(tc.tile_pool(name="keep", bufs=1))
         psum = ctx.enter_context(tc.psum_pool(name="psum", bufs=1))
@@ -70,50 +69,39 @@ def tile_mix_jvp_fm_pl_mul_kernel(tc, w, xd, wd, x, g, out_0, out_1, out_2):
             nc.sync.dma_start(out=tile[:], in_=rows(moving[step % 2], step))
             raw["x", step] = tile[:]
 
-        def load_weights(step, first, count):
-            pool, tag = (narrow, "narrow") if count == 1 else (wide, "wide")
-            tile = pool.tile([P, PACK, count * SPAN], F32, name="w_raw_%d_%d" % (step, first), tag=tag)
-            cols = slice(first * SPAN, (first + count) * SPAN)
-            nc.sync.dma_start(out=tile[:], in_=rows(weights[step % 2], step)[:, :, cols])
-            for i in range(count):
-                raw["w", step, first + i] = tile[:, :, i * SPAN : (i + 1) * SPAN]
+        def load_weights(step):
+            tile = wide.tile([P, PACK, M], F32, name="w_raw_%d" % step, tag="wide")
+            nc.sync.dma_start(out=tile[:], in_=rows(weights[step % 2], step))
+            for a in range(GROUPS):
+                raw["w", step, a] = tile[:, :, a * SPAN : (a + 1) * SPAN]
 
-        def load_last_early():
-            tile = wide.tile([P, 6 * M], F32, name="w_raw_last", tag="wide")
-            flat = weights[1][(K - SPAN) :, :].rearrange("(p j) n -> p (j n)", j=PACK)
-            run = 2 * M + 2 * SPAN
+        def load_last_weights_head():
+            tile = wide.tile([P, PACK * M], F32, name="w_raw_last", tag="wide")
+            flat = weights[LAST % 2][K - SPAN :, :].rearrange("(p j) n -> p (j n)", j=PACK)
+            run = PACK * M - SPAN
             nc.sync.dma_start(out=tile[:, :run], in_=flat[:, :run])
-            nc.sync.dma_start(out=tile[:, 3 * M : 3 * M + 2 * SPAN], in_=flat[:, 3 * M : 3 * M + 2 * SPAN])
-            view = tile[:].rearrange("p (j n) -> p j n", n=M)
-            for a in range(2):
-                raw["w", STEPS - 1, a] = view[:, :PACK, a * SPAN : (a + 1) * SPAN]
-            raw["last"] = view
-            raw["pairs"] = tile[:].rearrange("p (u v n) -> p u v n", u=2, v=3)
+            view = tile[:].rearrange("p (j n) -> p j n", j=PACK)
+            for a in range(GROUPS):
+                raw["w", LAST, a] = view[:, :, a * SPAN : (a + 1) * SPAN]
 
-        def load_last_late():
-            nc.sync.dma_start(out=raw["last"][:, 3:5, 2 * SPAN :], in_=rows(weights[1], STEPS - 1)[:, 2:, 2 * SPAN :])
-
-        def round_last():
-            key = ("w", STEPS - 1, 2)
-            tile = rounded.tile([P, SPAN * PACK], BF16, name="bf_w_last", tag="bf", align_bytes=64)
-            dealt = tile[:].rearrange("p (r m u v) -> p m u v r", r=PACK, u=2, v=2)
-            for copy, lo, hi in halves:
-                part = slice(lo // P, hi // P)
-                pairs = raw["pairs"][:, :, :2, 2 * SPAN :].rearrange("p u v (m r) -> p m u v r", r=PACK)
-                copy(out=dealt[:, :, :, :, part], in_=pairs[:, :, :, :, part])
-            bf[key] = tile
+        def load_last_weights_tail():
+            nc.sync.dma_start(
+                out=raw["w", LAST, 2][:, PACK - 1 :, :], in_=rows(weights[LAST % 2], LAST)[:, PACK - 1 :, M - SPAN :]
+            )
 
         def load_g(a):
             tile = keep.tile([P, PACK, T], F32, name="res_%d" % a)
             nc.sync.dma_start(out=tile[:], in_=g[a * SPAN : (a + 1) * SPAN, :].rearrange("(p r) t -> p r t", r=PACK))
             res[a] = tile
 
-        def round_plain(key, src, shares):
+        def rounded_tile(key):
             if key not in bf:
-                bf[key] = rounded.tile(
-                    [P, T * PACK], BF16, name="bf_" + "_".join(map(str, key)), tag="bf", align_bytes=64
-                )
-            tile = bf[key]
+                name = "bf_" + "_".join(map(str, key))
+                bf[key] = rounded.tile([P, SPAN * PACK], BF16, name=name, tag="bf", align_bytes=64)
+            return bf[key]
+
+        def round_plain(key, src, shares):
+            tile = rounded_tile(key)
             for copy, lo, hi in shares:
                 copy(
                     out=tile[:, lo * PACK : hi * PACK].rearrange("p (c i j) -> p c j i", i=4, j=PACK),
@@ -126,42 +114,42 @@ def tile_mix_jvp_fm_pl_mul_kernel(tc, w, xd, wd, x, g, out_0, out_1, out_2):
         def round_result(a, shares):
             round_plain(("o", a), res[a][:], shares)
 
-        def round_weights(step, a, shares, quads=slice(0, P)):
+        def round_weights(step, a, copy, quads=slice(0, P)):
             key = ("w", step, a)
-            if key not in bf:
-                bf[key] = rounded.tile(
-                    [P, SPAN * PACK], BF16, name="bf_w_%d_%d" % (step, a), tag="bf", align_bytes=64
-                )
-            tile = bf[key]
-            dealt = tile[:].rearrange("p (r m j) -> p m j r", r=PACK, j=PACK)
+            dealt = rounded_tile(key)[:].rearrange("p (r m j) -> p m j r", r=PACK, j=PACK)
             source = raw[key].rearrange("p j (m r) -> p m j r", r=PACK)
-            for copy, lo, hi in shares:
-                part = slice(lo // P, hi // P)
-                copy(out=dealt[:, quads, :, part], in_=source[:, quads, :, part])
+            copy(out=dealt[:, quads], in_=source[:, quads])
 
-        def quantize(key, fmt, plane=None):
-            label = "_".join(map(str, key))
-            home, tags = (passing, ("codes", "scales")) if key[0] == "w" and key[2] < 2 else (keep, (None, None))
-            words = home.tile([P, SPAN], U32, name="codes_" + label, tag=tags[0] or "codes_" + label, align_bytes=64)
-            if plane is None:
-                own = home.tile([P, SPAN], U8, name="scales_" + label, tag=tags[1] or "scales_" + label, align_bytes=64)
-                plane = own[:]
-            nc.vector.quantize_mx(out=words[:].bitcast(fmt), scales=plane, in_=bf[key][:])
-            codes[key] = words
-            scales[key] = plane
+        def code_tile(key):
+            codes[key] = keep.tile([P, SPAN], U32, name="codes_" + "_".join(map(str, key)), align_bytes=64)
+            return codes[key]
+
+        def quantize_operand(key, fmt):
+            words = code_tile(key)
+            scales[key] = keep.tile([P, SPAN], U8, name="scales_" + "_".join(map(str, key)), align_bytes=64)
+            nc.vector.quantize_mx(out=words[:].bitcast(fmt), scales=scales[key][:], in_=bf[key][:])
 
         def quantize_moving(step):
-            quantize(("x", step), moving_format[step % 2])
+            quantize_operand(("x", step), moving_format[step % 2])
 
         def quantize_weights(step, a):
-            quantize(("w", step, a), weight_format[step % 2])
+            quantize_operand(("w", step, a), weight_format[step % 2])
 
-        def quantize_result(a):
-            quantize(("o", a), E4M3, out_scales[:, a, :])
+        def hand_on_words(a, pieces):
+            words = code_tile(("o", a))
+            width = T // pieces
+            for lo in range(0, T, width):
+                cols = slice(lo, lo + width)
+                nc.vector.quantize_mx(
+                    out=words[:, cols].bitcast(E4M3),
+                    scales=out_scales[:, a, cols],
+                    in_=bf["o", a][:, lo * PACK : (lo + width) * PACK],
+                )
+                dst = out_1[a, :, cols, :].rearrange("p t i -> p (t i)").bitcast(I32)
+                nc.sync.dma_start(out=dst, in_=words[:, cols].bitcast(I32))
 
-        def multiply(a, r, step, last):
-            first = (a, r) not in acc
-            if first:
+        def multiply(a, r, step):
+            if step == 0:
                 bank = (a % 2) * PACK + r
                 acc[a, r] = psum.tile([P, T], F32, name="acc_%d_%d" % (a, r), tag="bank_%d" % bank)
             cols = slice(r * P, (r + 1) * P)
@@ -170,109 +158,108 @@ def tile_mix_jvp_fm_pl_mul_kernel(tc, w, xd, wd, x, g, out_0, out_1, out_2):
                 lhsT=codes["w", step, a][:, cols].bitcast(weight_format[step % 2]),
                 lhsT_scale=scales["w", step, a][:, cols],
                 rhs=codes["x", step][:].bitcast(moving_format[step % 2]),
-                rhs_scale=scales["x", step],
-                start=first,
-                stop=last,
+                rhs_scale=scales["x", step][:],
+                start=step == 0,
+                stop=step == LAST,
             )
 
-        def multiply_group(a, step, last=False):
+        def multiply_group(a, step):
             for r in range(PACK):
-                multiply(a, r, step, last)
+                multiply(a, r, step)
 
         def gate(a, r):
             nc.vector.tensor_tensor(
                 out=res[a][:, r, :], in0=acc[a, r][:], in1=res[a][:, r, :], op=mybir.AluOpType.mult
             )
 
-        def store_result(a, lo=0, hi=PACK):
+        def store_result(a, lo, hi):
             rows_out = out_0[a * SPAN : (a + 1) * SPAN, :].rearrange("(p r) t -> p r t", r=PACK)
             nc.sync.dma_start(out=rows_out[:, lo:hi, :], in_=res[a][:, lo:hi, :])
 
-        def store_words(a):
-            dst = out_1[a].rearrange("p t i -> p (t i)").bitcast(I32)
-            nc.sync.dma_start(out=dst, in_=codes["o", a][:].bitcast(I32))
-
         def store_scales():
-            for r in range(4):
-                dst = out_2.rearrange("a (q r) t -> r q a t", r=4)[r].bitcast(I32)
-                nc.sync.dma_start(out=dst, in_=out_scales[r:P:32, :, :].bitcast(I32))
+            for i in range(4):
+                dst = out_2.rearrange("a (q i) t -> i q a t", i=4)[i].bitcast(I32)
+                nc.sync.dma_start(out=dst, in_=out_scales[i:P:QUADRANT, :, :].bitcast(I32))
 
-        for step in range(3):
+        for step in range(LOADS_AHEAD):
             load_moving(step)
-            load_weights(step, 0, GROUPS)
+            load_weights(step)
 
         round_moving(0, all_scalar)
         quantize_moving(0)
-        for step in range(4):
-            round_weights(step, 0, all_vector)
-            round_weights(step, 1, all_scalar)
-            round_weights(step, 2, all_vector)
+        for step in range(LAST - 1):
+            next_is_streamed = step + 1 < LAST - 1
+            round_weights(step, 0, on_vector)
+            round_weights(step, 1, on_scalar)
+            round_weights(step, 2, on_vector)
             quantize_weights(step, 0)
             multiply_group(0, step)
             quantize_weights(step, 1)
             multiply_group(1, step)
-            round_moving(step + 1, all_scalar if step < 3 else [(on_scalar, 0, HELD)])
+            if next_is_streamed:
+                round_moving(step + 1, all_scalar)
             quantize_weights(step, 2)
-            if step < 3:
+            if next_is_streamed:
                 quantize_moving(step + 1)
-            if step < 2:
-                load_moving(step + 3)
-                load_weights(step + 3, 0, GROUPS)
-            if step == 2:
-                load_last_early()
-                load_moving(5)
+            if step + LOADS_AHEAD < LAST:
+                load_moving(step + LOADS_AHEAD)
+                load_weights(step + LOADS_AHEAD)
+            if step + LOADS_AHEAD == LAST:
+                load_last_weights_head()
+                load_moving(LAST)
                 load_g(0)
-                load_last_late()
+                load_last_weights_tail()
                 load_g(1)
                 load_g(2)
 
-        round_weights(4, 0, all_vector)
-        round_weights(4, 1, all_scalar)
-        round_moving(4, [(on_scalar, HELD, T)])
-        round_weights(4, 2, all_vector)
+        round_weights(LAST - 1, 0, on_vector)
+        round_weights(LAST - 1, 1, on_scalar)
+        round_moving(LAST - 1, all_scalar)
+        round_weights(LAST - 1, 2, on_vector)
         for a in (0, 2, 1):
-            quantize_weights(4, a)
-        quantize_moving(4)
-        multiply_group(0, 4)
-        multiply_group(1, 4)
-        round_weights(5, 0, all_vector)
-        round_weights(5, 1, all_scalar, slice(0, 96))
-        quantize_weights(5, 0)
-        round_moving(5, split_at(352))
-        round_weights(5, 1, all_scalar, slice(96, P))
-        quantize_moving(5)
-        multiply_group(0, 5, last=True)
-        quantize_weights(5, 1)
-        multiply_group(1, 5, last=True)
+            quantize_weights(LAST - 1, a)
+        quantize_moving(LAST - 1)
+        multiply_group(0, LAST - 1)
+        multiply_group(1, LAST - 1)
+
+        round_weights(LAST, 0, on_vector)
+        round_weights(LAST, 1, on_scalar, slice(0, EARLY_QUADS))
+        quantize_weights(LAST, 0)
+        round_moving(LAST, split_at(EVEN_SHARE))
+        round_weights(LAST, 1, on_scalar, slice(EARLY_QUADS, P))
+        quantize_moving(LAST)
+        multiply_group(0, LAST)
+        quantize_weights(LAST, 1)
+        multiply_group(1, LAST)
+        round_weights(LAST, 2, on_scalar)
+
         for r in range(PACK):
             gate(0, r)
-        store_result(0)
-        round_last()
+        store_result(0, 0, PACK)
         round_result(0, all_scalar)
-        quantize_weights(5, 2)
-        for r in range(2):
-            for step in range(STEPS - 1):
-                multiply(2, r, step, False)
-        for r in range(2):
-            multiply(2, r, STEPS - 1, True)
-        for r in range(2, PACK):
-            for step in range(STEPS):
-                multiply(2, r, step, step == STEPS - 1)
         for r in range(PACK):
             gate(1, r)
-        store_result(1)
-        round_result(1, split_at(128))
-        quantize_result(0)
-        store_words(0)
+        store_result(1, 0, PACK)
+        quantize_weights(LAST, 2)
+
         for r in range(PACK - 1):
-            gate(2, r)
-            if r == 1:
-                store_result(2, 0, 2)
-        quantize_result(1)
-        store_words(1)
-        gate(2, PACK - 1)
-        store_result(2, 2, 4)
-        round_result(2, both)
-        quantize_result(2)
-        store_words(2)
+            for step in range(LAST):
+                multiply(2, r, step)
+        for r in range(PACK - 1):
+            multiply(2, r, LAST)
+        for step in range(STEPS):
+            multiply(2, PACK - 1, step)
+
+        round_result(1, split_at(HELP_SHARE))
+        hand_on_words(0, 1)
+        gate(2, 0)
+        gate(2, 1)
+        store_result(2, 0, 2)
+        gate(2, 2)
+        hand_on_words(1, 1)
+        gate(2, 3)
+        store_result(2, 2, PACK)
+
+        round_result(2, [(on_scalar, EVEN_SHARE, T), (on_vector, 0, HALF), (on_vector, HALF, EVEN_SHARE)])
+        hand_on_words(2, 2)
         store_scales()

@@ -22,6 +22,7 @@ LAST = STEPS - 1
 LOADS_AHEAD = 3
 QUADRANT = 32
 HALF = T // 2
+DMA_ALIGN = 256
 
 EVEN_SHARE = 352
 HELP_SHARE = 128
@@ -58,25 +59,25 @@ def tile_mix_jvp_fm_pl_mul_kernel(tc, w, xd, wd, x, g, out_0, out_1, out_2):
         acc = {}
         res = {}
 
-        out_scales = keep.tile([P, GROUPS, T], U8, name="out_scales", align_bytes=64)
+        out_scales = keep.tile([P, GROUPS, T], U8, name="out_scales", align_bytes=DMA_ALIGN)
 
         def rows(src, step):
             c = step // 2
             return src[c * SPAN : (c + 1) * SPAN, :].rearrange("(p j) n -> p j n", j=PACK)
 
         def load_moving(step):
-            tile = narrow.tile([P, PACK, T], F32, name="x_raw_%d" % step, tag="narrow")
+            tile = narrow.tile([P, PACK, T], F32, name="x_raw_%d" % step, tag="narrow", align_bytes=DMA_ALIGN)
             nc.sync.dma_start(out=tile[:], in_=rows(moving[step % 2], step))
             raw["x", step] = tile[:]
 
         def load_weights(step):
-            tile = wide.tile([P, PACK, M], F32, name="w_raw_%d" % step, tag="wide")
+            tile = wide.tile([P, PACK, M], F32, name="w_raw_%d" % step, tag="wide", align_bytes=DMA_ALIGN)
             nc.sync.dma_start(out=tile[:], in_=rows(weights[step % 2], step))
             for a in range(GROUPS):
                 raw["w", step, a] = tile[:, :, a * SPAN : (a + 1) * SPAN]
 
         def load_last_weights_head():
-            tile = wide.tile([P, PACK * M], F32, name="w_raw_last", tag="wide")
+            tile = wide.tile([P, PACK * M], F32, name="w_raw_last", tag="wide", align_bytes=DMA_ALIGN)
             flat = weights[LAST % 2][K - SPAN :, :].rearrange("(p j) n -> p (j n)", j=PACK)
             run = PACK * M - SPAN
             nc.sync.dma_start(out=tile[:, :run], in_=flat[:, :run])
@@ -90,7 +91,7 @@ def tile_mix_jvp_fm_pl_mul_kernel(tc, w, xd, wd, x, g, out_0, out_1, out_2):
             )
 
         def load_g(a):
-            tile = keep.tile([P, PACK, T], F32, name="res_%d" % a)
+            tile = keep.tile([P, PACK, T], F32, name="res_%d" % a, align_bytes=DMA_ALIGN)
             nc.sync.dma_start(out=tile[:], in_=g[a * SPAN : (a + 1) * SPAN, :].rearrange("(p r) t -> p r t", r=PACK))
             res[a] = tile
 
@@ -121,7 +122,7 @@ def tile_mix_jvp_fm_pl_mul_kernel(tc, w, xd, wd, x, g, out_0, out_1, out_2):
             copy(out=dealt[:, quads], in_=source[:, quads])
 
         def code_tile(key):
-            codes[key] = keep.tile([P, SPAN], U32, name="codes_" + "_".join(map(str, key)), align_bytes=64)
+            codes[key] = keep.tile([P, SPAN], U32, name="codes_" + "_".join(map(str, key)), align_bytes=DMA_ALIGN)
             return codes[key]
 
         def quantize_operand(key, fmt):

@@ -22,9 +22,10 @@ LAST = STEPS - 1
 LOADS_AHEAD = 3
 QUADRANT = 32
 HALF = T // 2
-DMA_ALIGN = 256
+DMA_ALIGN = 2048
 
-EVEN_SHARE = 352
+MOVING_SHARE = 320
+LAST_SHARE = 160
 HELP_SHARE = 128
 EARLY_QUADS = 96
 
@@ -122,7 +123,7 @@ def tile_mix_jvp_fm_pl_mul_kernel(tc, w, xd, wd, x, g, out_0, out_1, out_2):
             copy(out=dealt[:, quads], in_=source[:, quads])
 
         def code_tile(key):
-            codes[key] = keep.tile([P, SPAN], U32, name="codes_" + "_".join(map(str, key)), align_bytes=DMA_ALIGN)
+            codes[key] = keep.tile([P, SPAN], U32, name="codes_" + "_".join(map(str, key)), align_bytes=DMA_ALIGN if key[0] == "o" else 256)
             return codes[key]
 
         def quantize_operand(key, fmt):
@@ -132,6 +133,17 @@ def tile_mix_jvp_fm_pl_mul_kernel(tc, w, xd, wd, x, g, out_0, out_1, out_2):
 
         def quantize_moving(step):
             quantize_operand(("x", step), moving_format[step % 2])
+
+        def quantize_moving_halves(step):
+            key = ("x", step)
+            words = code_tile(key)
+            scales[key] = keep.tile([P, SPAN], U8, name="scales_x_%d" % step, align_bytes=64)
+            for lo in (0, HALF):
+                nc.vector.quantize_mx(
+                    out=words[:, lo : lo + HALF].bitcast(moving_format[step % 2]),
+                    scales=scales[key][:, lo : lo + HALF],
+                    in_=bf[key][:, lo * PACK : (lo + HALF) * PACK],
+                )
 
         def quantize_weights(step, a):
             quantize_operand(("w", step, a), weight_format[step % 2])
@@ -168,19 +180,19 @@ def tile_mix_jvp_fm_pl_mul_kernel(tc, w, xd, wd, x, g, out_0, out_1, out_2):
             for r in range(PACK):
                 multiply(a, r, step)
 
-        def gate(a, r):
+        def gate(a, r, cols=slice(0, T)):
             nc.vector.tensor_tensor(
-                out=res[a][:, r, :], in0=acc[a, r][:], in1=res[a][:, r, :], op=mybir.AluOpType.mult
+                out=res[a][:, r, cols], in0=acc[a, r][:, cols], in1=res[a][:, r, cols], op=mybir.AluOpType.mult
             )
 
         def store_result(a, lo, hi):
             rows_out = out_0[a * SPAN : (a + 1) * SPAN, :].rearrange("(p r) t -> p r t", r=PACK)
             nc.sync.dma_start(out=rows_out[:, lo:hi, :], in_=res[a][:, lo:hi, :])
 
-        def store_scales():
+        def store_scales(groups, queues):
             for i in range(4):
-                dst = out_2.rearrange("a (q i) t -> i q a t", i=4)[i].bitcast(I32)
-                nc.sync.dma_start(out=dst, in_=out_scales[i:P:QUADRANT, :, :].bitcast(I32))
+                dst = out_2.rearrange("a (q i) t -> i q a t", i=4)[i][:, groups, :].bitcast(I32)
+                queues[i % len(queues)].dma_start(out=dst, in_=out_scales[i:P:QUADRANT, groups, :].bitcast(I32))
 
         for step in range(LOADS_AHEAD):
             load_moving(step)
@@ -226,9 +238,9 @@ def tile_mix_jvp_fm_pl_mul_kernel(tc, w, xd, wd, x, g, out_0, out_1, out_2):
         round_weights(LAST, 0, on_vector)
         round_weights(LAST, 1, on_scalar, slice(0, EARLY_QUADS))
         quantize_weights(LAST, 0)
-        round_moving(LAST, split_at(EVEN_SHARE))
+        round_moving(LAST, [(on_scalar, MOVING_SHARE, T), (on_vector, 0, HALF), (on_vector, HALF, MOVING_SHARE)])
         round_weights(LAST, 1, on_scalar, slice(EARLY_QUADS, P))
-        quantize_moving(LAST)
+        quantize_moving_halves(LAST)
         multiply_group(0, LAST)
         quantize_weights(LAST, 1)
         multiply_group(1, LAST)
@@ -258,9 +270,10 @@ def tile_mix_jvp_fm_pl_mul_kernel(tc, w, xd, wd, x, g, out_0, out_1, out_2):
         store_result(2, 0, 2)
         gate(2, 2)
         hand_on_words(1, 1)
-        gate(2, 3)
+        gate(2, 3, slice(0, HALF))
+        gate(2, 3, slice(HALF, T))
         store_result(2, 2, PACK)
 
-        round_result(2, [(on_scalar, EVEN_SHARE, T), (on_vector, 0, HALF), (on_vector, HALF, EVEN_SHARE)])
+        round_result(2, [(on_scalar, 0, LAST_SHARE), (on_vector, LAST_SHARE, HALF), (on_vector, HALF, T)])
         hand_on_words(2, 2)
-        store_scales()
+        store_scales(slice(0, GROUPS), [nc.scalar, nc.sync])

@@ -276,4 +276,4 @@ def tile_mix_jvp_fm_pl_mul_kernel(tc, w, xd, wd, x, g, out_0, out_1, out_2):
 
         round_result(2, [(on_scalar, 0, LAST_SHARE), (on_vector, LAST_SHARE, HALF), (on_vector, HALF, T)])
         hand_on_words(2, 2)
-        store_scales(slice(0, GROUPS), [nc.scalar, nc.sync])
+        store_scales(slice(0, GROUPS), [nc.sync])

@@ -12,6 +12,7 @@ I32 = mybir.dt.int32
 U8 = mybir.dt.uint8
 E4M3 = mybir.dt.float8_e4m3fn_x4
 E5M2 = mybir.dt.float8_e5m2_x4
+ALU = mybir.AluOpType
 
 P = 128
 PACK = 4
@@ -19,13 +20,16 @@ SPAN = P * PACK
 GROUPS = M // SPAN
 STEPS = 2 * (K // SPAN)
 LAST = STEPS - 1
-LOADS_AHEAD = 3
 QUADRANT = 32
+BANKS = 8
 HALF = T // 2
-DMA_ALIGN = 2048
+PAIRS = T * PACK // 2
+CHUNKS = PAIRS // P
+DMA_ALIGN = 256
 
 MOVING_SHARE = 320
 LAST_SHARE = 160
+SECOND_SHARE = 64
 HELP_SHARE = 128
 EARLY_QUADS = 96
 
@@ -34,11 +38,7 @@ def tile_mix_jvp_fm_pl_mul_kernel(tc, w, xd, wd, x, g, out_0, out_1, out_2):
     nc = tc.nc
     on_vector = nc.vector.tensor_copy
     on_scalar = nc.scalar.copy
-
-    all_scalar = [(on_scalar, 0, T)]
-
-    def split_at(column):
-        return [(on_scalar, column, T), (on_vector, 0, column)]
+    in_turn = [on_scalar, on_vector]
 
     weights = [w, wd]
     moving = [xd, x]
@@ -46,8 +46,8 @@ def tile_mix_jvp_fm_pl_mul_kernel(tc, w, xd, wd, x, g, out_0, out_1, out_2):
     moving_format = [E5M2, E4M3]
 
     with ExitStack() as ctx:
-        wide = ctx.enter_context(tc.tile_pool(name="wide", bufs=LOADS_AHEAD))
-        narrow = ctx.enter_context(tc.tile_pool(name="narrow", bufs=LOADS_AHEAD))
+        wide = ctx.enter_context(tc.tile_pool(name="wide", bufs=3))
+        narrow = ctx.enter_context(tc.tile_pool(name="narrow", bufs=1))
         rounded = ctx.enter_context(tc.tile_pool(name="rounded", bufs=6))
         keep = ctx.enter_context(tc.tile_pool(name="keep", bufs=1))
         psum = ctx.enter_context(tc.psum_pool(name="psum", bufs=1))
@@ -59,12 +59,27 @@ def tile_mix_jvp_fm_pl_mul_kernel(tc, w, xd, wd, x, g, out_0, out_1, out_2):
         scales = {}
         acc = {}
         res = {}
+        banks_used = []
 
         out_scales = keep.tile([P, GROUPS, T], U8, name="out_scales", align_bytes=DMA_ALIGN)
+
+        def bank_tile(bank, name):
+            return psum.tile([P, T], F32, name=name, tag="bank_%d" % bank)
+
+        def next_bank():
+            banks_used.append(len(banks_used))
+            return bank_tile(banks_used[-1] % BANKS, "turn_%d" % banks_used[-1])
 
         def rows(src, step):
             c = step // 2
             return src[c * SPAN : (c + 1) * SPAN, :].rearrange("(p j) n -> p j n", j=PACK)
+
+        def load_long(i, count, pool, tag):
+            tile = pool.tile([P, count, PACK, T], F32, name="x_long_%d" % i, tag=tag, align_bytes=DMA_ALIGN)
+            src = moving[i][: count * SPAN, :].rearrange("(p c j) t -> p c j t", c=count, j=PACK)
+            nc.sync.dma_start(out=tile[:], in_=src)
+            for c in range(count):
+                raw["long", i, c] = tile[:, c]
 
         def load_moving(step):
             tile = narrow.tile([P, PACK, T], F32, name="x_raw_%d" % step, tag="narrow", align_bytes=DMA_ALIGN)
@@ -110,68 +125,49 @@ def tile_mix_jvp_fm_pl_mul_kernel(tc, w, xd, wd, x, g, out_0, out_1, out_2):
                     in_=src[:, :, lo:hi].rearrange("p j (c i) -> p c j i", i=4),
                 )
 
-        def round_moving(step, shares):
-            round_plain(("x", step), raw["x", step], shares)
-
-        def round_result(a, shares):
-            round_plain(("o", a), res[a][:], shares)
-
         def round_weights(step, a, copy, quads=slice(0, P)):
             key = ("w", step, a)
             dealt = rounded_tile(key)[:].rearrange("p (r m j) -> p m j r", r=PACK, j=PACK)
             source = raw[key].rearrange("p j (m r) -> p m j r", r=PACK)
             copy(out=dealt[:, quads], in_=source[:, quads])
 
-        def code_tile(key):
-            codes[key] = keep.tile([P, SPAN], U32, name="codes_" + "_".join(map(str, key)), align_bytes=DMA_ALIGN if key[0] == "o" else 256)
-            return codes[key]
-
-        def quantize_operand(key, fmt):
-            words = code_tile(key)
-            scales[key] = keep.tile([P, SPAN], U8, name="scales_" + "_".join(map(str, key)), align_bytes=64)
-            nc.vector.quantize_mx(out=words[:].bitcast(fmt), scales=scales[key][:], in_=bf[key][:])
-
-        def quantize_moving(step):
-            quantize_operand(("x", step), moving_format[step % 2])
-
-        def quantize_moving_halves(step):
-            key = ("x", step)
-            words = code_tile(key)
-            scales[key] = keep.tile([P, SPAN], U8, name="scales_x_%d" % step, align_bytes=64)
-            for lo in (0, HALF):
+        def quantize(key, fmt, pieces=1, plane=None):
+            align = DMA_ALIGN
+            codes[key] = keep.tile([P, SPAN], U32, name="codes_" + "_".join(map(str, key)), align_bytes=align)
+            if plane is None:
+                plane = keep.tile([P, SPAN], U8, name="scales_" + "_".join(map(str, key)), align_bytes=64)[:]
+            scales[key] = plane
+            width = SPAN // pieces
+            for lo in range(0, SPAN, width):
                 nc.vector.quantize_mx(
-                    out=words[:, lo : lo + HALF].bitcast(moving_format[step % 2]),
-                    scales=scales[key][:, lo : lo + HALF],
-                    in_=bf[key][:, lo * PACK : (lo + HALF) * PACK],
+                    out=codes[key][:, lo : lo + width].bitcast(fmt),
+                    scales=plane[:, lo : lo + width],
+                    in_=bf[key][:, lo * PACK : (lo + width) * PACK],
                 )
+
+        def quantize_moving(step, pieces=1):
+            quantize(("x", step), moving_format[step % 2], pieces)
 
         def quantize_weights(step, a):
-            quantize_operand(("w", step, a), weight_format[step % 2])
+            quantize(("w", step, a), weight_format[step % 2])
 
-        def hand_on_words(a, pieces):
-            words = code_tile(("o", a))
+        def hand_on_words(a, pieces=1):
+            quantize(("o", a), E4M3, pieces, out_scales[:, a, :])
             width = T // pieces
             for lo in range(0, T, width):
-                cols = slice(lo, lo + width)
-                nc.vector.quantize_mx(
-                    out=words[:, cols].bitcast(E4M3),
-                    scales=out_scales[:, a, cols],
-                    in_=bf["o", a][:, lo * PACK : (lo + width) * PACK],
-                )
-                dst = out_1[a, :, cols, :].rearrange("p t i -> p (t i)").bitcast(I32)
-                nc.sync.dma_start(out=dst, in_=words[:, cols].bitcast(I32))
+                dst = out_1[a, :, lo : lo + width, :].rearrange("p t i -> p (t i)").bitcast(I32)
+                nc.sync.dma_start(out=dst, in_=codes["o", a][:, lo : lo + width].bitcast(I32))
 
         def multiply(a, r, step):
             if step == 0:
-                bank = (a % 2) * PACK + r
-                acc[a, r] = psum.tile([P, T], F32, name="acc_%d_%d" % (a, r), tag="bank_%d" % bank)
+                acc[a, r] = bank_tile((a % 2) * PACK + r, "acc_%d_%d" % (a, r))
             cols = slice(r * P, (r + 1) * P)
             nc.tensor.matmul_mx(
                 out=acc[a, r][:],
                 lhsT=codes["w", step, a][:, cols].bitcast(weight_format[step % 2]),
                 lhsT_scale=scales["w", step, a][:, cols],
                 rhs=codes["x", step][:].bitcast(moving_format[step % 2]),
-                rhs_scale=scales["x", step][:],
+                rhs_scale=scales["x", step],
                 start=step == 0,
                 stop=step == LAST,
             )
@@ -181,43 +177,85 @@ def tile_mix_jvp_fm_pl_mul_kernel(tc, w, xd, wd, x, g, out_0, out_1, out_2):
                 multiply(a, r, step)
 
         def gate(a, r, cols=slice(0, T)):
-            nc.vector.tensor_tensor(
-                out=res[a][:, r, cols], in0=acc[a, r][:, cols], in1=res[a][:, r, cols], op=mybir.AluOpType.mult
-            )
+            nc.vector.tensor_tensor(out=res[a][:, r, cols], in0=acc[a, r][:, cols], in1=res[a][:, r, cols], op=ALU.mult)
 
         def store_result(a, lo, hi):
             rows_out = out_0[a * SPAN : (a + 1) * SPAN, :].rearrange("(p r) t -> p r t", r=PACK)
             nc.sync.dma_start(out=rows_out[:, lo:hi, :], in_=res[a][:, lo:hi, :])
 
-        def store_scales(groups, queues):
-            for i in range(4):
-                dst = out_2.rearrange("a (q i) t -> i q a t", i=4)[i][:, groups, :].bitcast(I32)
-                queues[i % len(queues)].dma_start(out=dst, in_=out_scales[i:P:QUADRANT, groups, :].bitcast(I32))
+        def build_identity():
+            ones = keep.tile([P, P], F32, name="ones", align_bytes=64)
+            count = keep.tile([P, P], F32, name="count", align_bytes=64)
+            turned = keep.tile([P, P], F32, name="count_turned", align_bytes=64)
+            unit = keep.tile([P, P], F32, name="unit", align_bytes=64)
+            nc.vector.memset(ones[:], 1.0)
+            nc.vector.tensor_tensor_scan(
+                out=count[:], data0=ones[:], data1=ones[:], initial=0.0, op0=ALU.mult, op1=ALU.add
+            )
+            nc.vector.transpose(out=turned[:], in_=count[:])
+            for lo in range(0, P, QUADRANT):
+                part = slice(lo, lo + QUADRANT)
+                nc.vector.tensor_scalar(
+                    out=unit[part, :],
+                    in0=count[part, :],
+                    scalar1=turned[part, lo : lo + 1],
+                    scalar2=None,
+                    op0=ALU.is_equal,
+                )
+            return unit
 
-        for step in range(LOADS_AHEAD):
-            load_moving(step)
-            load_weights(step)
+        def deal(i, count):
+            across = narrow.tile([P, CHUNKS, count * P], F32, name="across_%d" % i, tag="across", align_bytes=64)
+            for h in range(CHUNKS):
+                bank = next_bank()
+                for c in range(count):
+                    pairs = bf["long", i, c][:].bitcast(F32)
+                    nc.tensor.transpose(bank[:, c * P : (c + 1) * P], pairs[:, h * P : (h + 1) * P], identity[:])
+                in_turn[h % 2](
+                    out=across[:, h, :].rearrange("f (p c) -> f p c", c=count),
+                    in_=bank[:, : count * P].rearrange("f (c p) -> f p c", c=count),
+                )
+            for s in range(count):
+                pairs = rounded_tile(("x", 2 * s + i))[:].bitcast(F32)
+                for half in range(2):
+                    bank = next_bank()
+                    for h in range(CHUNKS // 2):
+                        chunk = half * (CHUNKS // 2) + h
+                        nc.tensor.transpose(
+                            bank[:, h * P : (h + 1) * P], across[:, chunk, s * P : (s + 1) * P], identity[:]
+                        )
+                    in_turn[half](out=pairs[:, half * T : (half + 1) * T], in_=bank[:])
 
-        round_moving(0, all_scalar)
-        quantize_moving(0)
+        load_long(0, 3, wide, "wide")
+        load_long(1, 2, narrow, "narrow")
+        load_weights(0)
+        load_weights(1)
+        identity = build_identity()
+
+        for c, copy in enumerate([on_vector, on_scalar, on_vector]):
+            round_plain(("long", 0, c), raw["long", 0, c], [(copy, 0, T)])
+        load_weights(2)
+        deal(0, 3)
+        for c, copy in enumerate([on_vector, on_scalar]):
+            round_plain(("long", 1, c), raw["long", 1, c], [(copy, 0, T)])
+        for step in (0, 2, 4):
+            quantize_moving(step)
+        deal(1, 2)
+        for step in (1, 3):
+            quantize_moving(step)
+
         for step in range(LAST - 1):
-            next_is_streamed = step + 1 < LAST - 1
             round_weights(step, 0, on_vector)
             round_weights(step, 1, on_scalar)
             round_weights(step, 2, on_vector)
             quantize_weights(step, 0)
             multiply_group(0, step)
+            quantize_weights(step, 2)
             quantize_weights(step, 1)
             multiply_group(1, step)
-            if next_is_streamed:
-                round_moving(step + 1, all_scalar)
-            quantize_weights(step, 2)
-            if next_is_streamed:
-                quantize_moving(step + 1)
-            if step + LOADS_AHEAD < LAST:
-                load_moving(step + LOADS_AHEAD)
-                load_weights(step + LOADS_AHEAD)
-            if step + LOADS_AHEAD == LAST:
+            if step < 2:
+                load_weights(step + 3)
+            if step == 2:
                 load_last_weights_head()
                 load_moving(LAST)
                 load_g(0)
@@ -225,22 +263,21 @@ def tile_mix_jvp_fm_pl_mul_kernel(tc, w, xd, wd, x, g, out_0, out_1, out_2):
                 load_g(1)
                 load_g(2)
 
-        round_weights(LAST - 1, 0, on_vector)
-        round_weights(LAST - 1, 1, on_scalar)
-        round_moving(LAST - 1, all_scalar)
-        round_weights(LAST - 1, 2, on_vector)
-        for a in (0, 2, 1):
+        round_weights(LAST - 1, 1, on_vector)
+        round_weights(LAST - 1, 2, on_scalar)
+        round_weights(LAST - 1, 0, on_scalar)
+        for a in (1, 2, 0):
             quantize_weights(LAST - 1, a)
-        quantize_moving(LAST - 1)
         multiply_group(0, LAST - 1)
         multiply_group(1, LAST - 1)
 
         round_weights(LAST, 0, on_vector)
         round_weights(LAST, 1, on_scalar, slice(0, EARLY_QUADS))
         quantize_weights(LAST, 0)
-        round_moving(LAST, [(on_scalar, MOVING_SHARE, T), (on_vector, 0, HALF), (on_vector, HALF, MOVING_SHARE)])
+        shares = [(on_scalar, MOVING_SHARE, T), (on_vector, 0, HALF), (on_vector, HALF, MOVING_SHARE)]
+        round_plain(("x", LAST), raw["x", LAST], shares)
         round_weights(LAST, 1, on_scalar, slice(EARLY_QUADS, P))
-        quantize_moving_halves(LAST)
+        quantize_moving(LAST, 2)
         multiply_group(0, LAST)
         quantize_weights(LAST, 1)
         multiply_group(1, LAST)
@@ -249,7 +286,7 @@ def tile_mix_jvp_fm_pl_mul_kernel(tc, w, xd, wd, x, g, out_0, out_1, out_2):
         for r in range(PACK):
             gate(0, r)
         store_result(0, 0, PACK)
-        round_result(0, all_scalar)
+        round_plain(("o", 0), res[0][:], [(on_scalar, 0, T)])
         for r in range(PACK):
             gate(1, r)
         store_result(1, 0, PACK)
@@ -263,17 +300,25 @@ def tile_mix_jvp_fm_pl_mul_kernel(tc, w, xd, wd, x, g, out_0, out_1, out_2):
         for step in range(STEPS):
             multiply(2, PACK - 1, step)
 
-        round_result(1, split_at(HELP_SHARE))
-        hand_on_words(0, 1)
+        round_plain(("o", 1), res[1][:], [(on_scalar, HELP_SHARE, T), (on_vector, 0, HELP_SHARE)])
+        hand_on_words(0)
         gate(2, 0)
         gate(2, 1)
         store_result(2, 0, 2)
         gate(2, 2)
-        hand_on_words(1, 1)
+        hand_on_words(1)
         gate(2, 3, slice(0, HALF))
         gate(2, 3, slice(HALF, T))
         store_result(2, 2, PACK)
 
-        round_result(2, [(on_scalar, 0, LAST_SHARE), (on_vector, LAST_SHARE, HALF), (on_vector, HALF, T)])
+        shares = [
+            (on_scalar, 0, LAST_SHARE),
+            (on_vector, LAST_SHARE, HALF),
+            (on_scalar, HALF, HALF + SECOND_SHARE),
+            (on_vector, HALF + SECOND_SHARE, T),
+        ]
+        round_plain(("o", 2), res[2][:], shares)
         hand_on_words(2, 2)
-        store_scales(slice(0, GROUPS), [nc.sync])
+        for i in range(4):
+            dst = out_2.rearrange("a (q i) t -> i q a t", i=4)[i].bitcast(I32)
+            nc.sync.dma_start(out=dst, in_=out_scales[i:P:QUADRANT].bitcast(I32))

@@ -21,15 +21,16 @@ GROUPS = M // SPAN
 STEPS = 2 * (K // SPAN)
 LAST = STEPS - 1
 QUADRANT = 32
-BANKS = 8
 HALF = T // 2
 PAIRS = T * PACK // 2
-CHUNKS = PAIRS // P
+DEALT = 4
+SLAB_BYTES = PACK * T * 4
+LONG_PLACE, PACKED_PLACE, TURNED_PLACE = 0, 4, 6
+LATE_MOVING_PLACE = [3, 4]
 DMA_ALIGN = 256
 
 MOVING_SHARE = 320
-LAST_SHARE = 160
-SECOND_SHARE = 64
+LAST_SHARE = 128
 HELP_SHARE = 128
 EARLY_QUADS = 96
 
@@ -38,7 +39,6 @@ def tile_mix_jvp_fm_pl_mul_kernel(tc, w, xd, wd, x, g, out_0, out_1, out_2):
     nc = tc.nc
     on_vector = nc.vector.tensor_copy
     on_scalar = nc.scalar.copy
-    in_turn = [on_scalar, on_vector]
 
     weights = [w, wd]
     moving = [xd, x]
@@ -47,7 +47,7 @@ def tile_mix_jvp_fm_pl_mul_kernel(tc, w, xd, wd, x, g, out_0, out_1, out_2):
 
     with ExitStack() as ctx:
         wide = ctx.enter_context(tc.tile_pool(name="wide", bufs=3))
-        narrow = ctx.enter_context(tc.tile_pool(name="narrow", bufs=1))
+        room = ctx.enter_context(tc.tile_pool(name="room", bufs=1))
         rounded = ctx.enter_context(tc.tile_pool(name="rounded", bufs=6))
         keep = ctx.enter_context(tc.tile_pool(name="keep", bufs=1))
         psum = ctx.enter_context(tc.psum_pool(name="psum", bufs=1))
@@ -59,30 +59,27 @@ def tile_mix_jvp_fm_pl_mul_kernel(tc, w, xd, wd, x, g, out_0, out_1, out_2):
         scales = {}
         acc = {}
         res = {}
-        banks_used = []
 
         out_scales = keep.tile([P, GROUPS, T], U8, name="out_scales", align_bytes=DMA_ALIGN)
 
-        def bank_tile(bank, name):
-            return psum.tile([P, T], F32, name=name, tag="bank_%d" % bank)
-
-        def next_bank():
-            banks_used.append(len(banks_used))
-            return bank_tile(banks_used[-1] % BANKS, "turn_%d" % banks_used[-1])
+        def room_tile(name, shape, place):
+            return room.tile(shape, F32, name=name, align_bytes=DMA_ALIGN, offset=place * SLAB_BYTES)
 
         def rows(src, step):
             c = step // 2
             return src[c * SPAN : (c + 1) * SPAN, :].rearrange("(p j) n -> p j n", j=PACK)
 
-        def load_long(i, count, pool, tag):
-            tile = pool.tile([P, count, PACK, T], F32, name="x_long_%d" % i, tag=tag, align_bytes=DMA_ALIGN)
-            src = moving[i][: count * SPAN, :].rearrange("(p c j) t -> p c j t", c=count, j=PACK)
-            nc.sync.dma_start(out=tile[:], in_=src)
-            for c in range(count):
-                raw["long", i, c] = tile[:, c]
+        def load_long():
+            tile = room_tile("x_long", [P, DEALT, PACK, T], LONG_PLACE)
+            for step in range(DEALT):
+                c = step // 2
+                src = moving[step % 2][c * SPAN : (c + 1) * SPAN, :]
+                src = src.rearrange("(m u j) t -> m u j t", u=DEALT, j=PACK)
+                nc.sync.dma_start(out=tile[step:P:DEALT], in_=src)
+            raw["long"] = tile
 
         def load_moving(step):
-            tile = narrow.tile([P, PACK, T], F32, name="x_raw_%d" % step, tag="narrow", align_bytes=DMA_ALIGN)
+            tile = room_tile("x_raw_%d" % step, [P, PACK, T], LATE_MOVING_PLACE[step - DEALT])
             nc.sync.dma_start(out=tile[:], in_=rows(moving[step % 2], step))
             raw["x", step] = tile[:]
 
@@ -107,7 +104,7 @@ def tile_mix_jvp_fm_pl_mul_kernel(tc, w, xd, wd, x, g, out_0, out_1, out_2):
             )
 
         def load_g(a):
-            tile = keep.tile([P, PACK, T], F32, name="res_%d" % a, align_bytes=DMA_ALIGN)
+            tile = room_tile("res_%d" % a, [P, PACK, T], a)
             nc.sync.dma_start(out=tile[:], in_=g[a * SPAN : (a + 1) * SPAN, :].rearrange("(p r) t -> p r t", r=PACK))
             res[a] = tile
 
@@ -160,7 +157,8 @@ def tile_mix_jvp_fm_pl_mul_kernel(tc, w, xd, wd, x, g, out_0, out_1, out_2):
 
         def multiply(a, r, step):
             if step == 0:
-                acc[a, r] = bank_tile((a % 2) * PACK + r, "acc_%d_%d" % (a, r))
+                bank = (a % 2) * PACK + r
+                acc[a, r] = psum.tile([P, T], F32, name="acc_%d_%d" % (a, r), tag="bank_%d" % bank)
             cols = slice(r * P, (r + 1) * P)
             nc.tensor.matmul_mx(
                 out=acc[a, r][:],
@@ -183,68 +181,54 @@ def tile_mix_jvp_fm_pl_mul_kernel(tc, w, xd, wd, x, g, out_0, out_1, out_2):
             rows_out = out_0[a * SPAN : (a + 1) * SPAN, :].rearrange("(p r) t -> p r t", r=PACK)
             nc.sync.dma_start(out=rows_out[:, lo:hi, :], in_=res[a][:, lo:hi, :])
 
-        def build_identity():
-            ones = keep.tile([P, P], F32, name="ones", align_bytes=64)
-            count = keep.tile([P, P], F32, name="count", align_bytes=64)
-            turned = keep.tile([P, P], F32, name="count_turned", align_bytes=64)
-            unit = keep.tile([P, P], F32, name="unit", align_bytes=64)
-            nc.vector.memset(ones[:], 1.0)
-            nc.vector.tensor_tensor_scan(
-                out=count[:], data0=ones[:], data1=ones[:], initial=0.0, op0=ALU.mult, op1=ALU.add
-            )
-            nc.vector.transpose(out=turned[:], in_=count[:])
-            for lo in range(0, P, QUADRANT):
-                part = slice(lo, lo + QUADRANT)
-                nc.vector.tensor_scalar(
-                    out=unit[part, :],
-                    in0=count[part, :],
-                    scalar1=turned[part, lo : lo + 1],
-                    scalar2=None,
-                    op0=ALU.is_equal,
-                )
-            return unit
-
-        def deal(i, count):
-            across = narrow.tile([P, CHUNKS, count * P], F32, name="across_%d" % i, tag="across", align_bytes=64)
-            for h in range(CHUNKS):
-                bank = next_bank()
-                for c in range(count):
-                    pairs = bf["long", i, c][:].bitcast(F32)
-                    nc.tensor.transpose(bank[:, c * P : (c + 1) * P], pairs[:, h * P : (h + 1) * P], identity[:])
-                in_turn[h % 2](
-                    out=across[:, h, :].rearrange("f (p c) -> f p c", c=count),
-                    in_=bank[:, : count * P].rearrange("f (c p) -> f p c", c=count),
-                )
-            for s in range(count):
-                pairs = rounded_tile(("x", 2 * s + i))[:].bitcast(F32)
-                for half in range(2):
-                    bank = next_bank()
-                    for h in range(CHUNKS // 2):
-                        chunk = half * (CHUNKS // 2) + h
-                        nc.tensor.transpose(
-                            bank[:, h * P : (h + 1) * P], across[:, chunk, s * P : (s + 1) * P], identity[:]
-                        )
-                    in_turn[half](out=pairs[:, half * T : (half + 1) * T], in_=bank[:])
-
-        load_long(0, 3, wide, "wide")
-        load_long(1, 2, narrow, "narrow")
         load_weights(0)
+        load_long()
         load_weights(1)
-        identity = build_identity()
-
-        for c, copy in enumerate([on_vector, on_scalar, on_vector]):
-            round_plain(("long", 0, c), raw["long", 0, c], [(copy, 0, T)])
         load_weights(2)
-        deal(0, 3)
-        for c, copy in enumerate([on_vector, on_scalar]):
-            round_plain(("long", 1, c), raw["long", 1, c], [(copy, 0, T)])
-        for step in (0, 2, 4):
-            quantize_moving(step)
-        deal(1, 2)
-        for step in (1, 3):
-            quantize_moving(step)
 
-        for step in range(LAST - 1):
+        round_weights(0, 0, on_vector)
+        round_weights(0, 1, on_scalar)
+        round_weights(0, 2, on_vector)
+        for a in (0, 2, 1):
+            quantize_weights(0, a)
+        load_weights(3)
+
+        packed = room_tile("packed", [P, DEALT, PAIRS], PACKED_PLACE)
+        for u, copy in [(0, on_vector), (2, on_scalar), (1, on_vector), (3, on_scalar)]:
+            copy(
+                out=packed[:, u, :].bitcast(BF16).rearrange("p (c i j) -> p c j i", i=4, j=PACK),
+                in_=raw["long"][:, u].rearrange("p j (c i) -> p c j i", i=4),
+            )
+        turned = room_tile("turned", [P, DEALT, PAIRS], TURNED_PLACE)
+        for u in range(DEALT):
+            nc.vector.transpose(out=turned[:, u, :], in_=packed[:, u, :])
+        swapped = room_tile("swapped", [P, DEALT, PAIRS], PACKED_PLACE)
+        on_scalar(
+            out=swapped[:].rearrange("p s (y u) -> p y u s", u=DEALT),
+            in_=turned[:].rearrange("p u (y s) -> p y u s", s=DEALT),
+        )
+
+        def turn_back(step):
+            nc.vector.transpose(out=rounded_tile(("x", step))[:].bitcast(F32), in_=swapped[:, step, :])
+
+        round_weights(1, 0, on_vector)
+        round_weights(1, 2, on_vector)
+        round_weights(1, 1, on_scalar)
+        quantize_weights(1, 0)
+        quantize_weights(1, 2)
+        load_moving(LAST - 1)
+        load_weights(LAST - 1)
+        turn_back(0)
+        for step in range(1, DEALT):
+            turn_back(step)
+            quantize_moving(step - 1)
+        quantize_weights(1, 1)
+        quantize_moving(DEALT - 1)
+        for step in range(2):
+            multiply_group(0, step)
+            multiply_group(1, step)
+
+        for step in range(2, LAST - 1):
             round_weights(step, 0, on_vector)
             round_weights(step, 1, on_scalar)
             round_weights(step, 2, on_vector)
@@ -253,8 +237,6 @@ def tile_mix_jvp_fm_pl_mul_kernel(tc, w, xd, wd, x, g, out_0, out_1, out_2):
             quantize_weights(step, 2)
             quantize_weights(step, 1)
             multiply_group(1, step)
-            if step < 2:
-                load_weights(step + 3)
             if step == 2:
                 load_last_weights_head()
                 load_moving(LAST)
@@ -263,11 +245,13 @@ def tile_mix_jvp_fm_pl_mul_kernel(tc, w, xd, wd, x, g, out_0, out_1, out_2):
                 load_g(1)
                 load_g(2)
 
-        round_weights(LAST - 1, 1, on_vector)
-        round_weights(LAST - 1, 2, on_scalar)
-        round_weights(LAST - 1, 0, on_scalar)
-        for a in (1, 2, 0):
+        round_weights(LAST - 1, 0, on_vector)
+        round_weights(LAST - 1, 1, on_scalar)
+        round_plain(("x", LAST - 1), raw["x", LAST - 1], [(on_scalar, 0, T)])
+        round_weights(LAST - 1, 2, on_vector)
+        for a in (0, 2, 1):
             quantize_weights(LAST - 1, a)
+        quantize_moving(LAST - 1)
         multiply_group(0, LAST - 1)
         multiply_group(1, LAST - 1)
 
@@ -307,15 +291,15 @@ def tile_mix_jvp_fm_pl_mul_kernel(tc, w, xd, wd, x, g, out_0, out_1, out_2):
         store_result(2, 0, 2)
         gate(2, 2)
         hand_on_words(1)
-        gate(2, 3, slice(0, HALF))
-        gate(2, 3, slice(HALF, T))
+        gate(2, 3, slice(0, LAST_SHARE))
+        gate(2, 3, slice(LAST_SHARE, T))
         store_result(2, 2, PACK)
 
         shares = [
             (on_scalar, 0, LAST_SHARE),
             (on_vector, LAST_SHARE, HALF),
-            (on_scalar, HALF, HALF + SECOND_SHARE),
-            (on_vector, HALF + SECOND_SHARE, T),
+            (on_scalar, HALF, HALF + LAST_SHARE),
+            (on_vector, HALF + LAST_SHARE, T),
         ]
         round_plain(("o", 2), res[2][:], shares)
         hand_on_words(2, 2)

@@ -150,10 +150,8 @@ def tile_mix_jvp_fm_pl_mul_kernel(tc, w, xd, wd, x, g, out_0, out_1, out_2):
 
         def hand_on_words(a, pieces=1):
             quantize(("o", a), E4M3, pieces, out_scales[:, a, :])
-            width = T // pieces
-            for lo in range(0, T, width):
-                dst = out_1[a, :, lo : lo + width, :].rearrange("p t i -> p (t i)").bitcast(I32)
-                nc.sync.dma_start(out=dst, in_=codes["o", a][:, lo : lo + width].bitcast(I32))
+            dst = out_1[a].rearrange("p t i -> p (t i)").bitcast(I32)
+            nc.sync.dma_start(out=dst, in_=codes["o", a][:].bitcast(I32))
 
         def multiply(a, r, step):
             if step == 0:

from contextlib import ExitStack

import concourse.mybir as mybir

K, M, T = 1536, 1536, 512
FLOPS = 2 * 2 * K * M * T

F32 = mybir.dt.float32
BF16 = mybir.dt.bfloat16
U32 = mybir.dt.uint32
I32 = mybir.dt.int32
U8 = mybir.dt.uint8
E4M3 = mybir.dt.float8_e4m3fn_x4
E5M2 = mybir.dt.float8_e5m2_x4
ALU = mybir.AluOpType

P = 128
PACK = 4
SPAN = P * PACK
GROUPS = M // SPAN
STEPS = 2 * (K // SPAN)
LAST = STEPS - 1
QUADRANT = 32
HALF = T // 2
PAIRS = T * PACK // 2
DEALT = 4
SLAB_BYTES = PACK * T * 4
LONG_PLACE, PACKED_PLACE, TURNED_PLACE = 0, 4, 6
LATE_MOVING_PLACE = [3, 4]
DMA_ALIGN = 256

MOVING_SHARE = 320
LAST_SHARE = 128
HELP_SHARE = 128
EARLY_QUADS = 96


def tile_mix_jvp_fm_pl_mul_kernel(tc, w, xd, wd, x, g, out_0, out_1, out_2):
    nc = tc.nc
    on_vector = nc.vector.tensor_copy
    on_scalar = nc.scalar.copy

    weights = [w, wd]
    moving = [xd, x]
    weight_format = [E4M3, E5M2]
    moving_format = [E5M2, E4M3]

    with ExitStack() as ctx:
        wide = ctx.enter_context(tc.tile_pool(name="wide", bufs=3))
        room = ctx.enter_context(tc.tile_pool(name="room", bufs=1))
        rounded = ctx.enter_context(tc.tile_pool(name="rounded", bufs=6))
        keep = ctx.enter_context(tc.tile_pool(name="keep", bufs=1))
        psum = ctx.enter_context(tc.psum_pool(name="psum", bufs=1))
        ctx.enter_context(tc.manual_schedule())

        raw = {}
        bf = {}
        codes = {}
        scales = {}
        acc = {}
        res = {}

        out_scales = keep.tile([P, GROUPS, T], U8, name="out_scales", align_bytes=DMA_ALIGN)

        def room_tile(name, shape, place):
            return room.tile(shape, F32, name=name, align_bytes=DMA_ALIGN, offset=place * SLAB_BYTES)

        def rows(src, step):
            c = step // 2
            return src[c * SPAN : (c + 1) * SPAN, :].rearrange("(p j) n -> p j n", j=PACK)

        def load_long():
            tile = room_tile("x_long", [P, DEALT, PACK, T], LONG_PLACE)
            for step in range(DEALT):
                c = step // 2
                src = moving[step % 2][c * SPAN : (c + 1) * SPAN, :]
                src = src.rearrange("(m u j) t -> m u j t", u=DEALT, j=PACK)
                nc.sync.dma_start(out=tile[step:P:DEALT], in_=src)
            raw["long"] = tile

        def load_moving(step):
            tile = room_tile("x_raw_%d" % step, [P, PACK, T], LATE_MOVING_PLACE[step - DEALT])
            nc.sync.dma_start(out=tile[:], in_=rows(moving[step % 2], step))
            raw["x", step] = tile[:]

        def load_weights(step):
            tile = wide.tile([P, PACK, M], F32, name="w_raw_%d" % step, tag="wide", align_bytes=DMA_ALIGN)
            nc.sync.dma_start(out=tile[:], in_=rows(weights[step % 2], step))
            for a in range(GROUPS):
                raw["w", step, a] = tile[:, :, a * SPAN : (a + 1) * SPAN]

        def load_last_weights_head():
            tile = wide.tile([P, PACK * M], F32, name="w_raw_last", tag="wide", align_bytes=DMA_ALIGN)
            flat = weights[LAST % 2][K - SPAN :, :].rearrange("(p j) n -> p (j n)", j=PACK)
            run = PACK * M - SPAN
            nc.sync.dma_start(out=tile[:, :run], in_=flat[:, :run])
            view = tile[:].rearrange("p (j n) -> p j n", j=PACK)
            for a in range(GROUPS):
                raw["w", LAST, a] = view[:, :, a * SPAN : (a + 1) * SPAN]

        def load_last_weights_tail():
            nc.sync.dma_start(
                out=raw["w", LAST, 2][:, PACK - 1 :, :], in_=rows(weights[LAST % 2], LAST)[:, PACK - 1 :, M - SPAN :]
            )

        def load_g(a):
            tile = room_tile("res_%d" % a, [P, PACK, T], a)
            nc.sync.dma_start(out=tile[:], in_=g[a * SPAN : (a + 1) * SPAN, :].rearrange("(p r) t -> p r t", r=PACK))
            res[a] = tile

        def rounded_tile(key):
            if key not in bf:
                name = "bf_" + "_".join(map(str, key))
                bf[key] = rounded.tile([P, SPAN * PACK], BF16, name=name, tag="bf", align_bytes=64)
            return bf[key]

        def round_plain(key, src, shares):
            tile = rounded_tile(key)
            for copy, lo, hi in shares:
                copy(
                    out=tile[:, lo * PACK : hi * PACK].rearrange("p (c i j) -> p c j i", i=4, j=PACK),
                    in_=src[:, :, lo:hi].rearrange("p j (c i) -> p c j i", i=4),
                )

        def round_weights(step, a, copy, quads=slice(0, P)):
            key = ("w", step, a)
            dealt = rounded_tile(key)[:].rearrange("p (r m j) -> p m j r", r=PACK, j=PACK)
            source = raw[key].rearrange("p j (m r) -> p m j r", r=PACK)
            copy(out=dealt[:, quads], in_=source[:, quads])

        def quantize(key, fmt, pieces=1, plane=None):
            align = DMA_ALIGN
            codes[key] = keep.tile([P, SPAN], U32, name="codes_" + "_".join(map(str, key)), align_bytes=align)
            if plane is None:
                plane = keep.tile([P, SPAN], U8, name="scales_" + "_".join(map(str, key)), align_bytes=64)[:]
            scales[key] = plane
            width = SPAN // pieces
            for lo in range(0, SPAN, width):
                nc.vector.quantize_mx(
                    out=codes[key][:, lo : lo + width].bitcast(fmt),
                    scales=plane[:, lo : lo + width],
                    in_=bf[key][:, lo * PACK : (lo + width) * PACK],
                )

        def quantize_moving(step, pieces=1):
            quantize(("x", step), moving_format[step % 2], pieces)

        def quantize_weights(step, a):
            quantize(("w", step, a), weight_format[step % 2])

        def hand_on_words(a, pieces=1):
            quantize(("o", a), E4M3, pieces, out_scales[:, a, :])
            dst = out_1[a].rearrange("p t i -> p (t i)").bitcast(I32)
            nc.sync.dma_start(out=dst, in_=codes["o", a][:].bitcast(I32))

        def multiply(a, r, step):
            if step == 0:
                bank = (a % 2) * PACK + r
                acc[a, r] = psum.tile([P, T], F32, name="acc_%d_%d" % (a, r), tag="bank_%d" % bank)
            cols = slice(r * P, (r + 1) * P)
            nc.tensor.matmul_mx(
                out=acc[a, r][:],
                lhsT=codes["w", step, a][:, cols].bitcast(weight_format[step % 2]),
                lhsT_scale=scales["w", step, a][:, cols],
                rhs=codes["x", step][:].bitcast(moving_format[step % 2]),
                rhs_scale=scales["x", step],
                start=step == 0,
                stop=step == LAST,
            )

        def multiply_group(a, step):
            for r in range(PACK):
                multiply(a, r, step)

        def gate(a, r, cols=slice(0, T)):
            nc.vector.tensor_tensor(out=res[a][:, r, cols], in0=acc[a, r][:, cols], in1=res[a][:, r, cols], op=ALU.mult)

        def store_result(a, lo, hi):
            rows_out = out_0[a * SPAN : (a + 1) * SPAN, :].rearrange("(p r) t -> p r t", r=PACK)
            nc.sync.dma_start(out=rows_out[:, lo:hi, :], in_=res[a][:, lo:hi, :])

        load_weights(0)
        load_long()
        load_weights(1)
        load_weights(2)

        round_weights(0, 0, on_vector)
        round_weights(0, 1, on_scalar)
        round_weights(0, 2, on_vector)
        for a in (0, 2, 1):
            quantize_weights(0, a)
        load_weights(3)

        packed = room_tile("packed", [P, DEALT, PAIRS], PACKED_PLACE)
        for u, copy in [(0, on_vector), (2, on_scalar), (1, on_vector), (3, on_scalar)]:
            copy(
                out=packed[:, u, :].bitcast(BF16).rearrange("p (c i j) -> p c j i", i=4, j=PACK),
                in_=raw["long"][:, u].rearrange("p j (c i) -> p c j i", i=4),
            )
        turned = room_tile("turned", [P, DEALT, PAIRS], TURNED_PLACE)
        for u in range(DEALT):
            nc.vector.transpose(out=turned[:, u, :], in_=packed[:, u, :])
        swapped = room_tile("swapped", [P, DEALT, PAIRS], PACKED_PLACE)
        on_scalar(
            out=swapped[:].rearrange("p s (y u) -> p y u s", u=DEALT),
            in_=turned[:].rearrange("p u (y s) -> p y u s", s=DEALT),
        )

        def turn_back(step):
            nc.vector.transpose(out=rounded_tile(("x", step))[:].bitcast(F32), in_=swapped[:, step, :])

        round_weights(1, 0, on_vector)
        round_weights(1, 2, on_vector)
        round_weights(1, 1, on_scalar)
        quantize_weights(1, 0)
        quantize_weights(1, 2)
        load_moving(LAST - 1)
        load_weights(LAST - 1)
        turn_back(0)
        for step in range(1, DEALT):
            turn_back(step)
            quantize_moving(step - 1)
        quantize_weights(1, 1)
        quantize_moving(DEALT - 1)
        for step in range(2):
            multiply_group(0, step)
            multiply_group(1, step)

        for step in range(2, LAST - 1):
            round_weights(step, 0, on_vector)
            round_weights(step, 1, on_scalar)
            round_weights(step, 2, on_vector)
            quantize_weights(step, 0)
            multiply_group(0, step)
            quantize_weights(step, 2)
            quantize_weights(step, 1)
            multiply_group(1, step)
            if step == 2:
                load_last_weights_head()
                load_moving(LAST)
                load_g(0)
                load_last_weights_tail()
                load_g(1)
                load_g(2)

        round_weights(LAST - 1, 0, on_vector)
        round_weights(LAST - 1, 1, on_scalar)
        round_plain(("x", LAST - 1), raw["x", LAST - 1], [(on_scalar, 0, T)])
        round_weights(LAST - 1, 2, on_vector)
        for a in (0, 2, 1):
            quantize_weights(LAST - 1, a)
        quantize_moving(LAST - 1)
        multiply_group(0, LAST - 1)
        multiply_group(1, LAST - 1)

        round_weights(LAST, 0, on_vector)
        round_weights(LAST, 1, on_scalar, slice(0, EARLY_QUADS))
        quantize_weights(LAST, 0)
        shares = [(on_scalar, MOVING_SHARE, T), (on_vector, 0, HALF), (on_vector, HALF, MOVING_SHARE)]
        round_plain(("x", LAST), raw["x", LAST], shares)
        round_weights(LAST, 1, on_scalar, slice(EARLY_QUADS, P))
        quantize_moving(LAST, 2)
        multiply_group(0, LAST)
        quantize_weights(LAST, 1)
        multiply_group(1, LAST)
        round_weights(LAST, 2, on_scalar)

        for r in range(PACK):
            gate(0, r)
        store_result(0, 0, PACK)
        round_plain(("o", 0), res[0][:], [(on_scalar, 0, T)])
        for r in range(PACK):
            gate(1, r)
        store_result(1, 0, PACK)
        quantize_weights(LAST, 2)

        for r in range(PACK - 1):
            for step in range(LAST):
                multiply(2, r, step)
        for r in range(PACK - 1):
            multiply(2, r, LAST)
        for step in range(STEPS):
            multiply(2, PACK - 1, step)

        round_plain(("o", 1), res[1][:], [(on_scalar, HELP_SHARE, T), (on_vector, 0, HELP_SHARE)])
        hand_on_words(0)
        gate(2, 0)
        gate(2, 1)
        store_result(2, 0, 2)
        gate(2, 2)
        hand_on_words(1)
        gate(2, 3, slice(0, LAST_SHARE))
        gate(2, 3, slice(LAST_SHARE, T))
        store_result(2, 2, PACK)

        shares = [
            (on_scalar, 0, LAST_SHARE),
            (on_vector, LAST_SHARE, HALF),
            (on_scalar, HALF, HALF + LAST_SHARE),
            (on_vector, HALF + LAST_SHARE, T),
        ]
        round_plain(("o", 2), res[2][:], shares)
        hand_on_words(2, 2)
        for i in range(4):
            dst = out_2.rearrange("a (q i) t -> i q a t", i=4)[i].bitcast(I32)
            nc.sync.dma_start(out=dst, in_=out_scales[i:P:QUADRANT].bitcast(I32))
